import numpy as np
import ml_dtypes


def mxq(x, axis, fmt="e4m3"):
    dtype, down = {"e4m3": (ml_dtypes.float8_e4m3fn, 7), "e5m2": (ml_dtypes.float8_e5m2, 14)}[fmt]
    v = np.moveaxis(np.asarray(x, np.float32).astype(ml_dtypes.bfloat16).astype(np.float64), axis, -1)
    blocks = v.reshape(v.shape[:-1] + (-1, 32))
    amax = np.abs(blocks).max(-1, keepdims=True)
    byte = np.maximum(np.where(amax > 0, np.frexp(amax)[1] - 1 + 127, 0) - down, 1)
    scale = np.exp2(byte - 127.0)
    codes = (blocks / scale).astype(np.float32).astype(dtype).astype(np.float64)
    return np.moveaxis((codes * scale).reshape(v.shape), -1, axis)


WIDE = False


def mx_kscale(k):
    if not WIDE:
        return np.ones(k)
    levels = np.array([10, -10, 5, -5, 0])
    if k % 512:
        return np.exp2(np.random.permutation(np.resize(levels, k // 32))).repeat(32)
    a = np.empty((k // 512, 16))
    for p in range(k // 512):
        a[p, :8] = np.random.permutation(np.resize(levels, 8))
        for g in range(8):
            far = levels[np.abs(levels - a[p, g]) >= 10]
            a[p, g + 8] = far[np.random.randint(len(far))]
    return np.exp2(a.ravel()).repeat(32)


def f64(x):
    return np.asarray(x).astype(np.float64)


def striped8(idx):
    return np.concatenate([v.reshape(-1, 16).T for v in idx]).astype(np.uint16)


def unstriped8(offs):
    return np.stack([offs[16 * g:16 * g + 16].T.reshape(-1) for g in range(8)]).astype(np.int64)


E2M1 = np.array([0.0, 0.5, 1.0, 1.5, 2.0, 3.0, 4.0, 6.0, -0.0, -0.5, -1.0, -1.5, -2.0, -3.0, -4.0, -6.0])


def pack_weight(w, fmt):
    k, n = w.shape
    w = f64(np.asarray(w, np.float32).astype(ml_dtypes.bfloat16)).reshape(k // 32, 32, n)
    amax = np.abs(w).max(1)
    if fmt == "e4m3":
        byte = np.frexp(amax)[1] - 1 + 127 - 7
    else:
        mant, ex = np.frexp(amax / 6.0)
        byte = np.where(mant > 0.5, ex, ex - 1) + 127
    byte = np.clip(np.where(amax > 0, byte, 1), 1, 254)
    scaled = (w * np.exp2(127.0 - byte)[:, None, :]).reshape(k, n).astype(np.float32)
    by_word = np.ascontiguousarray(scaled.reshape(k // 512, 128, 4, n).transpose(0, 1, 3, 2))
    if fmt == "e4m3":
        words = by_word.astype(ml_dtypes.float8_e4m3fn).view(np.uint8)
    else:
        c = by_word.astype(ml_dtypes.float4_e2m1fn).view(np.uint8) & 0xF
        words = (c[..., 0::2] | (c[..., 1::2] << 4)).reshape(k // 512, 128, 2 * n)
    return np.ascontiguousarray(words), np.ascontiguousarray(byte.astype(np.uint8).reshape(k // 512, 16, n))


def unpack_weight(words, scales, fmt):
    g, _, n = scales.shape
    words = np.ascontiguousarray(words).reshape(g, 128, n, -1)
    if fmt == "e4m3":
        vals = words.view(ml_dtypes.float8_e4m3fn).astype(np.float64)
    else:
        nib = np.empty((g, 128, n, 4), np.uint8)
        nib[..., 0::2] = words & 0xF
        nib[..., 1::2] = words >> 4
        vals = E2M1[nib]
    vals = vals * np.repeat(np.exp2(scales.astype(np.float64) - 127.0), 8, axis=1)[..., None]
    return vals.transpose(0, 1, 3, 2).reshape(g * 512, n)


def gelu(v):
    return 0.5 * v * (1.0 + np.tanh(np.sqrt(2.0 / np.pi) * (v + 0.044715 * v**3)))


K, M, T, S = 1024, 1024, 1024, 512


def setup_inputs():
    n = np.random.standard_normal
    s = mx_kscale(K)[:, None]
    p_w = pack_weight(n((K, M)) / np.sqrt(K) / s, "e2m1")
    return {
        "x": (n((K, S)) * s).astype(np.float32),
        "w_words": p_w[0],
        "w_scales": p_w[1],
        "b": (0.3 * n(1024)).astype(np.float32),
        "wgo": np.repeat(np.random.uniform(0.5, 2.0, (8, S)), 16, axis=0).astype(np.float32),
        "offs": striped8(np.stack([np.random.permutation(T)[:S] for _ in range(8)])),
    }


def reference(x, w_words, w_scales, b, wgo, offs):
    x_ = mxq(f64(x), 0, "e4m3")
    w_ = unpack_weight(w_words, w_scales, "e2m1")
    y = w_.T @ x_
    place = unstriped8(offs)[np.arange(M) % 128 // 16]
    out = np.zeros((M, T))
    out[np.arange(M)[:, None], place] = f64(wgo)[np.arange(M) % 128] * (gelu(y + f64(b)[:, None]))
    return out

@@ -1,0 +1,161 @@
+from contextlib import ExitStack
+
+import concourse.mybir as mybir
+from concourse.masks import make_identity
+
+K, M, T, S = 1024, 1024, 1024, 512
+FLOPS = 2 * K * M * S
+
+F32 = mybir.dt.float32
+BF16 = mybir.dt.bfloat16
+I32 = mybir.dt.int32
+U32 = mybir.dt.uint32
+U16 = mybir.dt.uint16
+U8 = mybir.dt.uint8
+FP8X4 = mybir.dt.float8_e4m3fn_x4
+FP4X4 = mybir.dt.float4_e2m1fn_x4
+GELU = mybir.ActivationFunctionType.Gelu_apprx_tanh
+MULT = mybir.AluOpType.mult
+
+P = 128
+PASSES = K // 512
+TILES = M // P
+HALF = S // 2
+N_MM = 128
+EARLY = 2 * P // 2
+
+
+def interleave(copy, dst, src):
+    copy(
+        out=dst.rearrange("p (c i) t -> p c t i", i=4),
+        in_=src.rearrange("p t (c i) -> p c t i", i=4),
+    )
+
+
+def tile_list_hscat_gelu_kernel(tc, x, w_words, w_scales, b, wgo, offs, out):
+    nc = tc.nc
+    with ExitStack() as ctx:
+        keep = ctx.enter_context(tc.tile_pool(name="keep", bufs=1))
+        windows = ctx.enter_context(tc.tile_pool(name="windows", bufs=TILES))
+        vals = ctx.enter_context(tc.tile_pool(name="vals", bufs=4))
+        psum = ctx.enter_context(tc.psum_pool(name="psum", bufs=7))
+        psum_b = ctx.enter_context(tc.psum_pool(name="psum_b", bufs=1))
+
+        offsets = keep.tile([P, S // 16], U16, name="offsets")
+        wgo_sb = [keep.tile([P, HALF], F32, name=f"wgo{h}") for h in range(2)]
+        words = keep.tile([P, PASSES, 2 * M], U8, name="words", align_bytes=64)
+        planes = keep.tile([P, PASSES, M], U8, name="planes", align_bytes=64)
+        raw = [[keep.tile([P, 4, HALF], F32, name=f"raw{h}{a}") for a in range(PASSES)] for h in range(2)]
+        grouped = [keep.tile([P, PASSES, HALF, 4], BF16, name=f"grouped{h}", align_bytes=64) for h in range(2)]
+        codes = [keep.tile([P, PASSES, HALF], U32, name=f"codes{h}", align_bytes=64) for h in range(2)]
+        scales = [keep.tile([P, PASSES, HALF], U8, name=f"scales{h}", align_bytes=64) for h in range(2)]
+        warm = keep.tile([P, 1], F32, name="warm")
+        b_rows = keep.tile([P, P], F32, name="b_rows")
+        ident = keep.tile([P, P], F32, name="ident")
+        bias = keep.tile([P, TILES], F32, name="bias")
+
+        x_view = x.rearrange("(a p i) (h j) -> h a p i j", a=PASSES, i=4, h=2)
+        w_view = w_words.bitcast(I32).rearrange("a p n -> p a n")
+        s_view = w_scales.bitcast(I32).rearrange("a q n -> q a n")
+        words_i32 = words[:].rearrange("p a n -> p (a n)").bitcast(I32).rearrange("p (a n) -> p a n", a=PASSES)
+        planes_i32 = planes[:].rearrange("p a n -> p (a n)").bitcast(I32)
+        planes_i32_3 = planes_i32.rearrange("p (a n) -> p a n", a=PASSES)
+
+        wins = []
+
+        def new_window(engine):
+            win = windows.tile([P, T], F32, name="win")
+            engine.memset(win[:].bitcast(I32), 0)
+            wins.append(win)
+
+        nc.vector.memset(planes_i32, 0)
+        nc.gpsimd.memset(b_rows[:], 0.0)
+        make_identity(nc, ident[:])
+        nc.sync.dma_start(offsets[:], offs)
+        nc.scalar.dma_start(out=b_rows[0:TILES, :], in_=b.rearrange("(c p) -> c p", p=P))
+        nc.sync.dma_start(out=raw[0][0][:], in_=x_view[0, 0])
+        for q in range(4):
+            nc.sync.dma_start(out=planes_i32_3[32 * q : 32 * q + 4], in_=s_view[4 * q : 4 * q + 4])
+        nc.sync.dma_start(out=raw[0][1][:], in_=x_view[0, 1])
+        nc.sync.dma_start(out=words_i32[:, :, 0:EARLY], in_=w_view[:, :, 0:EARLY])
+        nc.sync.dma_start(out=wgo_sb[0][:], in_=wgo[:, 0:HALF])
+        nc.sync.dma_start(out=words_i32[:, :, EARLY:], in_=w_view[:, :, EARLY:])
+        nc.sync.dma_start(out=raw[1][0][:], in_=x_view[1, 0])
+        nc.sync.dma_start(out=raw[1][1][:], in_=x_view[1, 1])
+        nc.sync.dma_start(out=wgo_sb[1][:], in_=wgo[:, HALF:S])
+
+        for c in range(6):
+            new_window(nc.vector)
+        nc.scalar.activation(out=warm[:], in_=wins[0][:, 0:1], func=GELU)
+
+        b_t = psum_b.tile([P, P], F32, name="b_t")
+        nc.tensor.transpose(b_t[:], b_rows[:], ident[:])
+        nc.scalar.copy(out=bias[:], in_=b_t[:, 0:TILES])
+
+        def copy_piece(copy, h, a, j0, j1):
+            interleave(copy, grouped[h][:, a, j0:j1, :], raw[h][a][:, :, j0:j1])
+
+        def quantize_piece(h, a, j0, j1):
+            nc.vector.quantize_mx(
+                out=codes[h][:, a, j0:j1].bitcast(FP8X4),
+                scales=scales[h][:, a, j0:j1],
+                in_=grouped[h][:, a, j0:j1, :].rearrange("p j t -> p (j t)"),
+            )
+
+        def product(c, h):
+            val = vals.tile([P, HALF], F32, name="val")
+            for j0 in range(0, HALF, N_MM):
+                j1 = j0 + N_MM
+                acc = psum.tile([P, N_MM], F32, name="acc")
+                for a in range(PASSES):
+                    nc.tensor.matmul_mx(
+                        out=acc[:],
+                        lhsT=words[:, a, 2 * P * c : 2 * P * (c + 1)].bitcast(FP4X4),
+                        lhsT_scale=planes[:, a, P * c : P * (c + 1)],
+                        rhs=codes[h][:, a, j0:j1].bitcast(FP8X4),
+                        rhs_scale=scales[h][:, a, j0:j1],
+                        start=(a == 0),
+                        stop=(a == PASSES - 1),
+                    )
+                nc.scalar.activation(out=val[:, j0:j1], in_=acc[:], func=GELU, bias=bias[:, c : c + 1])
+            return val
+
+        def place(c, h, val):
+            nc.vector.tensor_tensor(
+                wins[c][:].indirect(offsets[:, 16 * h : 16 * (h + 1)]), val[:], wgo_sb[h][:], MULT
+            )
+
+        def finish(c):
+            place(c, 1, product(c, 1))
+            if c < TILES - 1:
+                nc.sync.dma_start(out=out[P * c : P * (c + 1), :], in_=wins[c][:])
+            else:
+                for queue, t0 in ((nc.sync, 0), (nc.scalar, T // 2)):
+                    queue.dma_start(out=out[P * c : P * (c + 1), t0 : t0 + T // 2], in_=wins[c][:, t0 : t0 + T // 2])
+
+        for a in range(PASSES):
+            copy_piece(nc.vector.tensor_copy, 0, a, 0, 128)
+            copy_piece(nc.scalar.copy, 0, a, 128, 256)
+            quantize_piece(0, a, 0, 128)
+            quantize_piece(0, a, 128, 256)
+        for c in range(2):
+            new_window(nc.vector)
+
+        place(0, 0, product(0, 0))
+        place(1, 0, product(1, 0))
+        for a in range(PASSES):
+            copy_piece(nc.scalar.copy, 1, a, 0, HALF)
+        nc.vector.quantize_mx(
+            out=codes[1][:].rearrange("p a j -> p (a j)").bitcast(FP8X4),
+            scales=scales[1][:].rearrange("p a j -> p (a j)"),
+            in_=grouped[1][:].rearrange("p a j t -> p (a j t)"),
+        )
+        place(2, 0, product(2, 0))
+        place(3, 0, product(3, 0))
+        for c in range(4):
+            finish(c)
+        for c in range(4, TILES, 2):
+            for e in (c, c + 1):
+                place(e, 0, product(e, 0))
+            for e in (c, c + 1):
+                finish(e)

@@ -1,7 +1,6 @@
 from contextlib import ExitStack
 
 import concourse.mybir as mybir
-from concourse.masks import make_identity
 
 K, M, T, S = 1024, 1024, 1024, 512
 FLOPS = 2 * K * M * S
@@ -20,9 +19,10 @@ MULT = mybir.AluOpType.mult
 P = 128
 PASSES = K // 512
 TILES = M // P
-HALF = S // 2
-N_MM = 128
-EARLY = 2 * P // 2
+PIECES = [(j, j + 128) for j in range(0, S, 128)]
+EARLY_TILES = 4
+WINDOWS = 4
+N_SMALL = 128
 
 
 def interleave(copy, dst, src):
@@ -36,126 +36,117 @@ def tile_list_hscat_gelu_kernel(tc, x, w_words, w_scales, b, wgo, offs, out):
     nc = tc.nc
     with ExitStack() as ctx:
         keep = ctx.enter_context(tc.tile_pool(name="keep", bufs=1))
-        windows = ctx.enter_context(tc.tile_pool(name="windows", bufs=TILES))
         vals = ctx.enter_context(tc.tile_pool(name="vals", bufs=4))
-        psum = ctx.enter_context(tc.psum_pool(name="psum", bufs=7))
-        psum_b = ctx.enter_context(tc.psum_pool(name="psum_b", bufs=1))
+        psum = ctx.enter_context(tc.psum_pool(name="psum", bufs=8))
 
         offsets = keep.tile([P, S // 16], U16, name="offsets")
-        wgo_sb = [keep.tile([P, HALF], F32, name=f"wgo{h}") for h in range(2)]
-        words = keep.tile([P, PASSES, 2 * M], U8, name="words", align_bytes=64)
         planes = keep.tile([P, PASSES, M], U8, name="planes", align_bytes=64)
-        raw = [[keep.tile([P, 4, HALF], F32, name=f"raw{h}{a}") for a in range(PASSES)] for h in range(2)]
-        grouped = [keep.tile([P, PASSES, HALF, 4], BF16, name=f"grouped{h}", align_bytes=64) for h in range(2)]
-        codes = [keep.tile([P, PASSES, HALF], U32, name=f"codes{h}", align_bytes=64) for h in range(2)]
-        scales = [keep.tile([P, PASSES, HALF], U8, name=f"scales{h}", align_bytes=64) for h in range(2)]
-        warm = keep.tile([P, 1], F32, name="warm")
-        b_rows = keep.tile([P, P], F32, name="b_rows")
-        ident = keep.tile([P, P], F32, name="ident")
+        codes = keep.tile([P, PASSES, S], U32, name="codes", align_bytes=64)
+        scales = keep.tile([P, PASSES, S], U8, name="scales", align_bytes=64)
+        wins = [keep.tile([P, T], F32, name=f"win{w}") for w in range(WINDOWS)]
+        warm = keep.tile([P, 2], F32, name="warm")
         bias = keep.tile([P, TILES], F32, name="bias")
+        wgo_first = keep.tile([P, PIECES[0][1]], F32, name="wgo_first", tag="wgo_first", align_bytes=64)
 
-        x_view = x.rearrange("(a p i) (h j) -> h a p i j", a=PASSES, i=4, h=2)
+        x_view = x.rearrange("(a p i) j -> a p i j", a=PASSES, i=4)
         w_view = w_words.bitcast(I32).rearrange("a p n -> p a n")
         s_view = w_scales.bitcast(I32).rearrange("a q n -> q a n")
-        words_i32 = words[:].rearrange("p a n -> p (a n)").bitcast(I32).rearrange("p (a n) -> p a n", a=PASSES)
         planes_i32 = planes[:].rearrange("p a n -> p (a n)").bitcast(I32)
         planes_i32_3 = planes_i32.rearrange("p (a n) -> p a n", a=PASSES)
 
-        wins = []
+        def load_x(n, a, tag):
+            j0, j1 = PIECES[n]
+            raw = keep.tile([P, 4, j1 - j0], F32, name=f"raw{n}{a}", tag=tag, align_bytes=64)
+            nc.sync.dma_start(out=raw[:], in_=x_view[a][:, :, j0:j1])
+            return raw
 
-        def new_window(engine):
-            win = windows.tile([P, T], F32, name="win")
-            engine.memset(win[:].bitcast(I32), 0)
-            wins.append(win)
+        def load_words(c0, c1, tag):
+            tile = keep.tile([P, PASSES, (c1 - c0) * P // 2], I32, name=f"words{c0}", tag=tag, align_bytes=64)
+            nc.sync.dma_start(out=tile[:], in_=w_view[:, :, c0 * P // 2 : c1 * P // 2])
+            return tile
 
-        nc.vector.memset(planes_i32, 0)
-        nc.gpsimd.memset(b_rows[:], 0.0)
-        make_identity(nc, ident[:])
+        nc.gpsimd.memset(planes_i32, 0)
+        nc.gpsimd.memset(warm[:, 0:1], 0.0)
         nc.sync.dma_start(offsets[:], offs)
-        nc.scalar.dma_start(out=b_rows[0:TILES, :], in_=b.rearrange("(c p) -> c p", p=P))
-        nc.sync.dma_start(out=raw[0][0][:], in_=x_view[0, 0])
+        raw = [[load_x(0, a, f"raw{a}") for a in range(PASSES)]]
         for q in range(4):
             nc.sync.dma_start(out=planes_i32_3[32 * q : 32 * q + 4], in_=s_view[4 * q : 4 * q + 4])
-        nc.sync.dma_start(out=raw[0][1][:], in_=x_view[0, 1])
-        nc.sync.dma_start(out=words_i32[:, :, 0:EARLY], in_=w_view[:, :, 0:EARLY])
-        nc.sync.dma_start(out=wgo_sb[0][:], in_=wgo[:, 0:HALF])
-        nc.sync.dma_start(out=words_i32[:, :, EARLY:], in_=w_view[:, :, EARLY:])
-        nc.sync.dma_start(out=raw[1][0][:], in_=x_view[1, 0])
-        nc.sync.dma_start(out=raw[1][1][:], in_=x_view[1, 1])
-        nc.sync.dma_start(out=wgo_sb[1][:], in_=wgo[:, HALF:S])
+        words_early = load_words(0, EARLY_TILES, "words_early")
+        with nc.allow_non_contiguous_dma(reason="one bias value to a partition and row tile"):
+            nc.sync.dma_start(out=bias[:], in_=b.rearrange("(c p) -> p c", p=P))
+        nc.sync.dma_start(out=wgo_first[:], in_=wgo[:, 0 : PIECES[0][1]])
 
-        for c in range(6):
-            new_window(nc.vector)
-        nc.scalar.activation(out=warm[:], in_=wins[0][:, 0:1], func=GELU)
+        for win in wins:
+            nc.vector.memset(win[:].bitcast(I32), 0)
+        nc.scalar.activation(out=warm[:, 1:2], in_=warm[:, 0:1], func=GELU)
 
-        b_t = psum_b.tile([P, P], F32, name="b_t")
-        nc.tensor.transpose(b_t[:], b_rows[:], ident[:])
-        nc.scalar.copy(out=bias[:], in_=b_t[:, 0:TILES])
+        def quantize(copy, n):
+            j0, j1 = PIECES[n]
+            for a in range(PASSES):
+                grouped = keep.tile([P, j1 - j0, 4], BF16, name=f"grouped{n}{a}", tag=f"grouped{n}{a}", align_bytes=64)
+                interleave(copy, grouped[:], raw[n][a][:])
+                nc.vector.quantize_mx(
+                    out=codes[:, a, j0:j1].bitcast(FP8X4),
+                    scales=scales[:, a, j0:j1],
+                    in_=grouped[:].rearrange("p j t -> p (j t)"),
+                )
 
-        def copy_piece(copy, h, a, j0, j1):
-            interleave(copy, grouped[h][:, a, j0:j1, :], raw[h][a][:, :, j0:j1])
+        quantize(nc.vector.tensor_copy, 0)
+        raw.append([load_x(1, a, f"raw{a}") for a in range(PASSES)])
+        wgo_sb = keep.tile([P, S], F32, name="wgo_sb", tag="grouped00", align_bytes=64)
+        nc.sync.dma_start(out=wgo_sb[:], in_=wgo)
+        raw.append([load_x(2, 0, "grouped01"), load_x(2, 1, "raw0")])
+        words_late = load_words(EARLY_TILES, TILES, "wgo_first")
 
-        def quantize_piece(h, a, j0, j1):
-            nc.vector.quantize_mx(
-                out=codes[h][:, a, j0:j1].bitcast(FP8X4),
-                scales=scales[h][:, a, j0:j1],
-                in_=grouped[h][:, a, j0:j1, :].rearrange("p j t -> p (j t)"),
-            )
-
-        def product(c, h):
-            val = vals.tile([P, HALF], F32, name="val")
-            for j0 in range(0, HALF, N_MM):
-                j1 = j0 + N_MM
-                acc = psum.tile([P, N_MM], F32, name="acc")
+        def product(c, j0, j1, val):
+            acc = psum.tile([P, S], F32, name="acc")
+            step = S if j1 - j0 == S else N_SMALL
+            words, first = (words_early, 0) if c < EARLY_TILES else (words_late, EARLY_TILES)
+            w0 = (c - first) * P // 2
+            for m0 in range(j0, j1, step):
                 for a in range(PASSES):
                     nc.tensor.matmul_mx(
-                        out=acc[:],
-                        lhsT=words[:, a, 2 * P * c : 2 * P * (c + 1)].bitcast(FP4X4),
+                        out=acc[:, m0 - j0 : m0 - j0 + step],
+                        lhsT=words[:, a, w0 : w0 + P // 2].bitcast(U8).bitcast(FP4X4),
                         lhsT_scale=planes[:, a, P * c : P * (c + 1)],
-                        rhs=codes[h][:, a, j0:j1].bitcast(FP8X4),
-                        rhs_scale=scales[h][:, a, j0:j1],
+                        rhs=codes[:, a, m0 : m0 + step].bitcast(FP8X4),
+                        rhs_scale=scales[:, a, m0 : m0 + step],
                         start=(a == 0),
                         stop=(a == PASSES - 1),
                     )
-                nc.scalar.activation(out=val[:, j0:j1], in_=acc[:], func=GELU, bias=bias[:, c : c + 1])
-            return val
+            nc.scalar.activation(out=val, in_=acc[:, 0 : j1 - j0], func=GELU, bias=bias[:, c : c + 1])
 
-        def place(c, h, val):
-            nc.vector.tensor_tensor(
-                wins[c][:].indirect(offsets[:, 16 * h : 16 * (h + 1)]), val[:], wgo_sb[h][:], MULT
-            )
+        def place(c, j0, j1, val=None):
+            if val is None:
+                fresh = vals.tile([P, S], F32, name="val")
+                val = fresh[:, 0 : j1 - j0]
+            product(c, j0, j1, val)
+            win = wins[c % WINDOWS]
+            weights = wgo_first[:] if j1 == PIECES[0][1] else wgo_sb[:, j0:j1]
+            nc.vector.tensor_tensor(win[:].indirect(offsets[:, j0 // 16 : j1 // 16]), val, weights, MULT)
+            if j1 == S:
+                rows = out[P * c : P * (c + 1), :]
+                if c < TILES - 1:
+                    nc.sync.dma_start(out=rows, in_=win[:])
+                else:
+                    for queue, t0 in ((nc.sync, 0), (nc.scalar, T // 2)):
+                        queue.dma_start(out=rows[:, t0 : t0 + T // 2], in_=win[:, t0 : t0 + T // 2])
 
-        def finish(c):
-            place(c, 1, product(c, 1))
-            if c < TILES - 1:
-                nc.sync.dma_start(out=out[P * c : P * (c + 1), :], in_=wins[c][:])
-            else:
-                for queue, t0 in ((nc.sync, 0), (nc.scalar, T // 2)):
-                    queue.dma_start(out=out[P * c : P * (c + 1), t0 : t0 + T // 2], in_=wins[c][:, t0 : t0 + T // 2])
+        def phase(n, tiles):
+            j0, j1 = PIECES[n]
+            for c in tiles[:-1]:
+                place(c, j0, j1)
+            quantize(nc.scalar.copy, n + 1)
+            if n == 0:
+                raw.append([load_x(3, a, f"grouped1{a}") for a in range(PASSES)])
+            place(tiles[-1], j0, j1, raw[n + 1][PASSES - 1][:, 0, :])
 
-        for a in range(PASSES):
-            copy_piece(nc.vector.tensor_copy, 0, a, 0, 128)
-            copy_piece(nc.scalar.copy, 0, a, 128, 256)
-            quantize_piece(0, a, 0, 128)
-            quantize_piece(0, a, 128, 256)
-        for c in range(2):
-            new_window(nc.vector)
-
-        place(0, 0, product(0, 0))
-        place(1, 0, product(1, 0))
-        for a in range(PASSES):
-            copy_piece(nc.scalar.copy, 1, a, 0, HALF)
-        nc.vector.quantize_mx(
-            out=codes[1][:].rearrange("p a j -> p (a j)").bitcast(FP8X4),
-            scales=scales[1][:].rearrange("p a j -> p (a j)"),
-            in_=grouped[1][:].rearrange("p a j t -> p (a j t)"),
-        )
-        place(2, 0, product(2, 0))
-        place(3, 0, product(3, 0))
-        for c in range(4):
-            finish(c)
-        for c in range(4, TILES, 2):
-            for e in (c, c + 1):
-                place(e, 0, product(e, 0))
-            for e in (c, c + 1):
-                finish(e)
+        phase(0, [0, 1, 2, 3])
+        phase(1, [0, 1, 2, 3])
+        phase(2, [0, 1])
+        for c in (0, 1):
+            place(c, *PIECES[3])
+        for c in (2, 3):
+            place(c, PIECES[2][0], S)
+        for c in range(EARLY_TILES, TILES):
+            place(c, 0, S)

@@ -41,10 +41,12 @@ def tile_list_hscat_gelu_kernel(tc, x, w_words, w_scales, b, wgo, offs, out):
 
         offsets = keep.tile([P, S // 16], U16, name="offsets")
         planes = keep.tile([P, PASSES, M], U8, name="planes", align_bytes=64)
-        codes = keep.tile([P, PASSES, S], U32, name="codes", align_bytes=64)
-        scales = keep.tile([P, PASSES, S], U8, name="scales", align_bytes=64)
-        wins = [keep.tile([P, T], F32, name=f"win{w}") for w in range(WINDOWS)]
+        codes = keep.tile([P, len(PIECES), PASSES, N_SMALL], U32, name="codes", align_bytes=64)
+        scales = keep.tile([P, len(PIECES), PASSES, N_SMALL], U8, name="scales", align_bytes=64)
+        wins = [keep.tile([P, T], F32, name=f"win{w}") for w in range(WINDOWS - 1)]
         warm = keep.tile([P, 2], F32, name="warm")
+        b_rows = keep.tile([P, P], F32, name="b_rows", align_bytes=64)
+        b_turned = keep.tile([P, P], F32, name="b_turned", align_bytes=64)
         bias = keep.tile([P, TILES], F32, name="bias")
         wgo_first = keep.tile([P, PIECES[0][1]], F32, name="wgo_first", tag="wgo_first", align_bytes=64)
 
@@ -67,41 +69,51 @@ def tile_list_hscat_gelu_kernel(tc, x, w_words, w_scales, b, wgo, offs, out):
 
         nc.gpsimd.memset(planes_i32, 0)
         nc.gpsimd.memset(warm[:, 0:1], 0.0)
-        nc.sync.dma_start(offsets[:], offs)
+        nc.sync.dma_start(
+            out=b_rows[:], in_=b.rearrange("(c p) -> c p", p=P).unsqueeze(0).to_broadcast([P // TILES, TILES, P])
+        )
         raw = [[load_x(0, a, f"raw{a}") for a in range(PASSES)]]
         for q in range(4):
             nc.sync.dma_start(out=planes_i32_3[32 * q : 32 * q + 4], in_=s_view[4 * q : 4 * q + 4])
         words_early = load_words(0, EARLY_TILES, "words_early")
-        with nc.allow_non_contiguous_dma(reason="one bias value to a partition and row tile"):
-            nc.sync.dma_start(out=bias[:], in_=b.rearrange("(c p) -> p c", p=P))
+        nc.sync.dma_start(offsets[:], offs)
         nc.sync.dma_start(out=wgo_first[:], in_=wgo[:, 0 : PIECES[0][1]])
 
+        nc.vector.transpose(b_turned[:], b_rows[:])
+        for u in range(4):
+            nc.scalar.copy(out=bias[32 * u : 32 * u + 32, :], in_=b_turned[32 * u : 32 * u + 32, 32 * u : 32 * u + TILES])
         for win in wins:
             nc.vector.memset(win[:].bitcast(I32), 0)
         nc.scalar.activation(out=warm[:, 1:2], in_=warm[:, 0:1], func=GELU)
 
-        def quantize(copy, n):
-            j0, j1 = PIECES[n]
-            for a in range(PASSES):
-                grouped = keep.tile([P, j1 - j0, 4], BF16, name=f"grouped{n}{a}", tag=f"grouped{n}{a}", align_bytes=64)
-                interleave(copy, grouped[:], raw[n][a][:])
-                nc.vector.quantize_mx(
-                    out=codes[:, a, j0:j1].bitcast(FP8X4),
-                    scales=scales[:, a, j0:j1],
-                    in_=grouped[:].rearrange("p j t -> p (j t)"),
-                )
+        def quantize(grouped, n, a0, a1):
+            nc.vector.quantize_mx(
+                out=codes[:, n, a0:a1, :].rearrange("p a j -> p (a j)").bitcast(FP8X4),
+                scales=scales[:, n, a0:a1, :].rearrange("p a j -> p (a j)"),
+                in_=grouped.rearrange("p a j t -> p (a j t)"),
+            )
 
-        quantize(nc.vector.tensor_copy, 0)
+        def quantize_later(n):
+            grouped = keep.tile([P, PASSES, N_SMALL, 4], BF16, name=f"grouped{n}", tag=f"grouped{n}", align_bytes=64)
+            for a in range(PASSES):
+                interleave(nc.scalar.copy, grouped[:, a], raw[n][a][:])
+            quantize(grouped[:], n, 0, PASSES)
+
+        for a in range(PASSES):
+            first = keep.tile([P, 1, N_SMALL, 4], BF16, name=f"grouped0{a}", tag=f"grouped0{a}", align_bytes=64)
+            interleave(nc.vector.tensor_copy, first[:, 0], raw[0][a][:])
+            quantize(first[:], 0, a, a + 1)
+        wins.append(keep.tile([P, T], F32, name="win_last", tag="grouped01", align_bytes=64))
+        nc.vector.memset(wins[-1][:].bitcast(I32), 0)
         raw.append([load_x(1, a, f"raw{a}") for a in range(PASSES)])
         wgo_sb = keep.tile([P, S], F32, name="wgo_sb", tag="grouped00", align_bytes=64)
         nc.sync.dma_start(out=wgo_sb[:], in_=wgo)
-        raw.append([load_x(2, 0, "grouped01"), load_x(2, 1, "raw0")])
-        words_late = load_words(EARLY_TILES, TILES, "wgo_first")
+        words_late = []
 
         def product(c, j0, j1, val):
             acc = psum.tile([P, S], F32, name="acc")
-            step = S if j1 - j0 == S else N_SMALL
-            words, first = (words_early, 0) if c < EARLY_TILES else (words_late, EARLY_TILES)
+            step = N_SMALL
+            words, first = (words_early, 0) if c < EARLY_TILES else (words_late[0], EARLY_TILES)
             w0 = (c - first) * P // 2
             for m0 in range(j0, j1, step):
                 for a in range(PASSES):
@@ -109,8 +121,8 @@ def tile_list_hscat_gelu_kernel(tc, x, w_words, w_scales, b, wgo, offs, out):
                         out=acc[:, m0 - j0 : m0 - j0 + step],
                         lhsT=words[:, a, w0 : w0 + P // 2].bitcast(U8).bitcast(FP4X4),
                         lhsT_scale=planes[:, a, P * c : P * (c + 1)],
-                        rhs=codes[:, a, m0 : m0 + step].bitcast(FP8X4),
-                        rhs_scale=scales[:, a, m0 : m0 + step],
+                        rhs=codes[:, m0 // step, a, :].bitcast(FP8X4),
+                        rhs_scale=scales[:, m0 // step, a, :],
                         start=(a == 0),
                         stop=(a == PASSES - 1),
                     )
@@ -136,10 +148,14 @@ def tile_list_hscat_gelu_kernel(tc, x, w_words, w_scales, b, wgo, offs, out):
             j0, j1 = PIECES[n]
             for c in tiles[:-1]:
                 place(c, j0, j1)
-            quantize(nc.scalar.copy, n + 1)
+            quantize_later(n + 1)
             if n == 0:
-                raw.append([load_x(3, a, f"grouped1{a}") for a in range(PASSES)])
+                raw.append([load_x(2, 0, "raw0"), load_x(2, 1, "grouped1")])
             place(tiles[-1], j0, j1, raw[n + 1][PASSES - 1][:, 0, :])
+            if n == 0:
+                raw.append([load_x(3, 0, "raw1"), load_x(3, 1, "wgo_first")])
+            if n == 1:
+                words_late.append(load_words(EARLY_TILES, TILES, "grouped2"))
 
         phase(0, [0, 1, 2, 3])
         phase(1, [0, 1, 2, 3])

@@ -38,6 +38,8 @@ def tile_list_hscat_gelu_kernel(tc, x, w_words, w_scales, b, wgo, offs, out):
         keep = ctx.enter_context(tc.tile_pool(name="keep", bufs=1))
         vals = ctx.enter_context(tc.tile_pool(name="vals", bufs=4))
         psum = ctx.enter_context(tc.psum_pool(name="psum", bufs=8))
+        slide = ctx.enter_context(tc.tile_pool(name="slide", bufs=1))
+        after = ctx.enter_context(tc.tile_pool(name="after", bufs=1))
 
         offsets = keep.tile([P, S // 16], U16, name="offsets")
         planes = keep.tile([P, PASSES, M], U8, name="planes", align_bytes=64)
@@ -56,9 +58,12 @@ def tile_list_hscat_gelu_kernel(tc, x, w_words, w_scales, b, wgo, offs, out):
         planes_i32 = planes[:].rearrange("p a n -> p (a n)").bitcast(I32)
         planes_i32_3 = planes_i32.rearrange("p (a n) -> p a n", a=PASSES)
 
-        def load_x(n, a, tag):
+        def load_x(n, a, tag=None, offset=None, pool=slide):
             j0, j1 = PIECES[n]
-            raw = keep.tile([P, 4, j1 - j0], F32, name=f"raw{n}{a}", tag=tag, align_bytes=64)
+            if tag is None:
+                raw = pool.tile([P, 4, j1 - j0], F32, name=f"raw{n}{a}", offset=offset, align_bytes=64)
+            else:
+                raw = keep.tile([P, 4, j1 - j0], F32, name=f"raw{n}{a}", tag=tag, align_bytes=64)
             nc.sync.dma_start(out=raw[:], in_=x_view[a][:, :, j0:j1])
             return raw
 
@@ -72,7 +77,7 @@ def tile_list_hscat_gelu_kernel(tc, x, w_words, w_scales, b, wgo, offs, out):
         nc.sync.dma_start(
             out=b_rows[:], in_=b.rearrange("(c p) -> c p", p=P).unsqueeze(0).to_broadcast([P // TILES, TILES, P])
         )
-        raw = [[load_x(0, a, f"raw{a}") for a in range(PASSES)]]
+        raw = [[load_x(0, 0, offset=2560), load_x(0, 1, tag="raw0")]]
         for q in range(4):
             nc.sync.dma_start(out=planes_i32_3[32 * q : 32 * q + 4], in_=s_view[4 * q : 4 * q + 4])
         words_early = load_words(0, EARLY_TILES, "words_early")
@@ -94,19 +99,25 @@ def tile_list_hscat_gelu_kernel(tc, x, w_words, w_scales, b, wgo, offs, out):
             )
 
         def quantize_later(n):
-            grouped = keep.tile([P, PASSES, N_SMALL, 4], BF16, name=f"grouped{n}", tag=f"grouped{n}", align_bytes=64)
+            if n == 1:
+                grouped = slide.tile([P, PASSES, N_SMALL, 4], BF16, name="grouped1", offset=7168, align_bytes=64)
+            else:
+                grouped = keep.tile([P, PASSES, N_SMALL, 4], BF16, name=f"grouped{n}", tag=f"grouped{n}", align_bytes=64)
             for a in range(PASSES):
                 interleave(nc.scalar.copy, grouped[:, a], raw[n][a][:])
             quantize(grouped[:], n, 0, PASSES)
 
+        firsts = [
+            keep.tile([P, 1, N_SMALL, 4], BF16, name="grouped00", align_bytes=64),
+            after.tile([P, 1, N_SMALL, 4], BF16, name="grouped01", offset=1536, align_bytes=64),
+        ]
         for a in range(PASSES):
-            first = keep.tile([P, 1, N_SMALL, 4], BF16, name=f"grouped0{a}", tag=f"grouped0{a}", align_bytes=64)
-            interleave(nc.vector.tensor_copy, first[:, 0], raw[0][a][:])
-            quantize(first[:], 0, a, a + 1)
-        wins.append(keep.tile([P, T], F32, name="win_last", tag="grouped01", align_bytes=64))
+            interleave(nc.vector.tensor_copy, firsts[a][:, 0], raw[0][a][:])
+            quantize(firsts[a][:], 0, a, a + 1)
+        wins.append(after.tile([P, T], F32, name="win_last", offset=2048, align_bytes=64))
         nc.vector.memset(wins[-1][:].bitcast(I32), 0)
-        raw.append([load_x(1, a, f"raw{a}") for a in range(PASSES)])
-        wgo_sb = keep.tile([P, S], F32, name="wgo_sb", tag="grouped00", align_bytes=64)
+        raw.append([load_x(1, 0, offset=1024), load_x(1, 1, offset=4096)])
+        wgo_sb = keep.tile([P, S], F32, name="wgo_sb", tag="raw0", align_bytes=64)
         nc.sync.dma_start(out=wgo_sb[:], in_=wgo)
         words_late = []
 
@@ -144,25 +155,26 @@ def tile_list_hscat_gelu_kernel(tc, x, w_words, w_scales, b, wgo, offs, out):
                     for queue, t0 in ((nc.sync, 0), (nc.scalar, T // 2)):
                         queue.dma_start(out=rows[:, t0 : t0 + T // 2], in_=win[:, t0 : t0 + T // 2])
 
-        def phase(n, tiles):
-            j0, j1 = PIECES[n]
-            for c in tiles[:-1]:
-                place(c, j0, j1)
-            quantize_later(n + 1)
-            if n == 0:
-                raw.append([load_x(2, 0, "raw0"), load_x(2, 1, "grouped1")])
-            place(tiles[-1], j0, j1, raw[n + 1][PASSES - 1][:, 0, :])
-            if n == 0:
-                raw.append([load_x(3, 0, "raw1"), load_x(3, 1, "wgo_first")])
-            if n == 1:
-                words_late.append(load_words(EARLY_TILES, TILES, "grouped2"))
+        def held(name, offset, width):
+            val = slide.tile([P, width], F32, name=name, offset=offset, align_bytes=64)
+            return val[:]
 
-        phase(0, [0, 1, 2, 3])
-        phase(1, [0, 1, 2, 3])
-        phase(2, [0, 1])
-        for c in (0, 1):
-            place(c, *PIECES[3])
-        for c in (2, 3):
-            place(c, PIECES[2][0], S)
+        place(0, 0, 128)
+        place(1, 0, 128)
+        quantize_later(1)
+        raw.append([load_x(2, 0, offset=0, pool=after), load_x(2, 1, offset=2048)])
+        raw.append([load_x(3, 0, offset=6144), load_x(3, 1, offset=8192)])
+        place(2, 0, 128, held("val20", 4096, 128))
+        place(3, 0, 128, held("val30", 4608, 128))
+        place(0, 128, 256)
+        quantize_later(2)
+        place(1, 128, 256, held("val11", 2048, 128))
+        place(2, 128, 256, held("val21", 2560, 128))
+        quantize_later(3)
+        words_late.append(load_words(EARLY_TILES, TILES, "grouped3"))
+        place(3, 128, 384, held("val31", 8192, 256))
+        for c in (0, 1, 2):
+            place(c, 256, S)
+        place(3, 384, S)
         for c in range(EARLY_TILES, TILES):
             place(c, 0, S)

@@ -167,14 +167,17 @@ def tile_list_hscat_gelu_kernel(tc, x, w_words, w_scales, b, wgo, offs, out):
         place(2, 0, 128, held("val20", 4096, 128))
         place(3, 0, 128, held("val30", 4608, 128))
         place(0, 128, 256)
+        place(1, 128, 256)
         quantize_later(2)
-        place(1, 128, 256, held("val11", 2048, 128))
-        place(2, 128, 256, held("val21", 2560, 128))
+        place(2, 128, 256, held("val21", 2048, 128))
+        place(3, 128, 256, held("val31", 2560, 128))
         quantize_later(3)
         words_late.append(load_words(EARLY_TILES, TILES, "grouped3"))
-        place(3, 128, 384, held("val31", 8192, 256))
-        for c in (0, 1, 2):
+        place(0, 256, 384, held("val02", 8192, 128))
+        place(1, 256, 384, held("val12", 8704, 128))
+        for c in (0, 1):
+            place(c, 384, S)
+        for c in (2, 3):
             place(c, 256, S)
-        place(3, 384, S)
         for c in range(EARLY_TILES, TILES):
             place(c, 0, S)

@@ -46,7 +46,7 @@ def tile_list_hscat_gelu_kernel(tc, x, w_words, w_scales, b, wgo, offs, out):
         codes = keep.tile([P, len(PIECES), PASSES, N_SMALL], U32, name="codes", align_bytes=64)
         scales = keep.tile([P, len(PIECES), PASSES, N_SMALL], U8, name="scales", align_bytes=64)
         wins = [keep.tile([P, T], F32, name=f"win{w}") for w in range(WINDOWS - 1)]
-        warm = keep.tile([P, 2], F32, name="warm")
+        warm = keep.tile([P, 1], F32, name="warm")
         b_rows = keep.tile([P, P], F32, name="b_rows", align_bytes=64)
         b_turned = keep.tile([P, P], F32, name="b_turned", align_bytes=64)
         bias = keep.tile([P, TILES], F32, name="bias")
@@ -73,7 +73,6 @@ def tile_list_hscat_gelu_kernel(tc, x, w_words, w_scales, b, wgo, offs, out):
             return tile
 
         nc.gpsimd.memset(planes_i32, 0)
-        nc.gpsimd.memset(warm[:, 0:1], 0.0)
         nc.sync.dma_start(
             out=b_rows[:], in_=b.rearrange("(c p) -> c p", p=P).unsqueeze(0).to_broadcast([P // TILES, TILES, P])
         )
@@ -89,7 +88,7 @@ def tile_list_hscat_gelu_kernel(tc, x, w_words, w_scales, b, wgo, offs, out):
             nc.scalar.copy(out=bias[32 * u : 32 * u + 32, :], in_=b_turned[32 * u : 32 * u + 32, 32 * u : 32 * u + TILES])
         for win in wins:
             nc.vector.memset(win[:].bitcast(I32), 0)
-        nc.scalar.activation(out=warm[:, 1:2], in_=warm[:, 0:1], func=GELU)
+        nc.scalar.activation(out=warm[:], in_=wins[0][:, 0:1], func=GELU)
 
         def quantize(grouped, n, a0, a1):
             nc.vector.quantize_mx(

@@ -19,10 +19,10 @@ MULT = mybir.AluOpType.mult
 P = 128
 PASSES = K // 512
 TILES = M // P
-PIECES = [(j, j + 128) for j in range(0, S, 128)]
-EARLY_TILES = 4
-WINDOWS = 4
-N_SMALL = 128
+N = 128
+PIECES = [(0, 128), (128, 256), (256, 512)]
+WORD_LOADS = [(0, 4), (4, 6), (6, 8)]
+WINDOWS = 6
 
 
 def interleave(copy, dst, src):
@@ -36,21 +36,20 @@ def tile_list_hscat_gelu_kernel(tc, x, w_words, w_scales, b, wgo, offs, out):
     nc = tc.nc
     with ExitStack() as ctx:
         keep = ctx.enter_context(tc.tile_pool(name="keep", bufs=1))
-        vals = ctx.enter_context(tc.tile_pool(name="vals", bufs=4))
         psum = ctx.enter_context(tc.psum_pool(name="psum", bufs=8))
-        slide = ctx.enter_context(tc.tile_pool(name="slide", bufs=1))
-        after = ctx.enter_context(tc.tile_pool(name="after", bufs=1))
+        late = ctx.enter_context(tc.tile_pool(name="late", bufs=1))
+        held = ctx.enter_context(tc.tile_pool(name="held", bufs=1))
 
         offsets = keep.tile([P, S // 16], U16, name="offsets")
         planes = keep.tile([P, PASSES, M], U8, name="planes", align_bytes=64)
-        codes = keep.tile([P, len(PIECES), PASSES, N_SMALL], U32, name="codes", align_bytes=64)
-        scales = keep.tile([P, len(PIECES), PASSES, N_SMALL], U8, name="scales", align_bytes=64)
-        wins = [keep.tile([P, T], F32, name=f"win{w}") for w in range(WINDOWS - 1)]
+        codes = [keep.tile([P, PASSES, j1 - j0], U32, name=f"codes{j0}", align_bytes=64) for j0, j1 in PIECES]
+        scales = [keep.tile([P, PASSES, j1 - j0], U8, name=f"scales{j0}", align_bytes=64) for j0, j1 in PIECES]
+        wins = [keep.tile([P, T], F32, name=f"win{w}") for w in range(3)]
         warm = keep.tile([P, 1], F32, name="warm")
         b_rows = keep.tile([P, P], F32, name="b_rows", align_bytes=64)
         b_turned = keep.tile([P, P], F32, name="b_turned", align_bytes=64)
         bias = keep.tile([P, TILES], F32, name="bias")
-        wgo_first = keep.tile([P, PIECES[0][1]], F32, name="wgo_first", tag="wgo_first", align_bytes=64)
+        weights = keep.tile([P, S], F32, name="weights", align_bytes=64)
 
         x_view = x.rearrange("(a p i) j -> a p i j", a=PASSES, i=4)
         w_view = w_words.bitcast(I32).rearrange("a p n -> p a n")
@@ -58,30 +57,38 @@ def tile_list_hscat_gelu_kernel(tc, x, w_words, w_scales, b, wgo, offs, out):
         planes_i32 = planes[:].rearrange("p a n -> p (a n)").bitcast(I32)
         planes_i32_3 = planes_i32.rearrange("p (a n) -> p a n", a=PASSES)
 
-        def load_x(n, a, tag=None, offset=None, pool=slide):
+        def load_x(n, a, offset):
             j0, j1 = PIECES[n]
-            if tag is None:
-                raw = pool.tile([P, 4, j1 - j0], F32, name=f"raw{n}{a}", offset=offset, align_bytes=64)
-            else:
-                raw = keep.tile([P, 4, j1 - j0], F32, name=f"raw{n}{a}", tag=tag, align_bytes=64)
+            raw = held.tile([P, 4, j1 - j0], F32, name=f"raw{n}{a}", offset=offset, align_bytes=64)
             nc.sync.dma_start(out=raw[:], in_=x_view[a][:, :, j0:j1])
             return raw
 
-        def load_words(c0, c1, tag):
-            tile = keep.tile([P, PASSES, (c1 - c0) * P // 2], I32, name=f"words{c0}", tag=tag, align_bytes=64)
+        words = {}
+
+        def load_words(c0, c1):
+            tile = keep.tile([P, PASSES, (c1 - c0) * P // 2], I32, name=f"words{c0}", align_bytes=64)
             nc.sync.dma_start(out=tile[:], in_=w_view[:, :, c0 * P // 2 : c1 * P // 2])
-            return tile
+            for c in range(c0, c1):
+                words[c] = tile[:, :, (c - c0) * P // 2 : (c - c0 + 1) * P // 2]
+
+        def load_weights(j0, j1):
+            nc.sync.dma_start(out=weights[:, j0:j1], in_=wgo[:, j0:j1])
 
         nc.gpsimd.memset(planes_i32, 0)
         nc.sync.dma_start(
             out=b_rows[:], in_=b.rearrange("(c p) -> c p", p=P).unsqueeze(0).to_broadcast([P // TILES, TILES, P])
         )
-        raw = [[load_x(0, 0, offset=2560), load_x(0, 1, tag="raw0")]]
+        raw = [[load_x(0, 0, 0), load_x(0, 1, 2048)]]
         for q in range(4):
             nc.sync.dma_start(out=planes_i32_3[32 * q : 32 * q + 4], in_=s_view[4 * q : 4 * q + 4])
-        words_early = load_words(0, EARLY_TILES, "words_early")
+        load_words(*WORD_LOADS[0])
         nc.sync.dma_start(offsets[:], offs)
-        nc.sync.dma_start(out=wgo_first[:], in_=wgo[:, 0 : PIECES[0][1]])
+        load_weights(0, N)
+        raw.append([load_x(1, 0, 4096), load_x(1, 1, 6144)])
+        load_words(*WORD_LOADS[1])
+        load_weights(N, S)
+        raw.append([load_x(2, 0, 8192), load_x(2, 1, 12288)])
+        load_words(*WORD_LOADS[2])
 
         nc.vector.transpose(b_turned[:], b_rows[:])
         for u in range(4):
@@ -92,60 +99,47 @@ def tile_list_hscat_gelu_kernel(tc, x, w_words, w_scales, b, wgo, offs, out):
 
         def quantize(grouped, n, a0, a1):
             nc.vector.quantize_mx(
-                out=codes[:, n, a0:a1, :].rearrange("p a j -> p (a j)").bitcast(FP8X4),
-                scales=scales[:, n, a0:a1, :].rearrange("p a j -> p (a j)"),
+                out=codes[n][:, a0:a1, :].rearrange("p a j -> p (a j)").bitcast(FP8X4),
+                scales=scales[n][:, a0:a1, :].rearrange("p a j -> p (a j)"),
                 in_=grouped.rearrange("p a j t -> p (a j t)"),
             )
 
-        def quantize_later(n):
-            if n == 1:
-                grouped = slide.tile([P, PASSES, N_SMALL, 4], BF16, name="grouped1", offset=7168, align_bytes=64)
-            else:
-                grouped = keep.tile([P, PASSES, N_SMALL, 4], BF16, name=f"grouped{n}", tag=f"grouped{n}", align_bytes=64)
+        def quantize_later(n, grouped):
             for a in range(PASSES):
                 interleave(nc.scalar.copy, grouped[:, a], raw[n][a][:])
             quantize(grouped[:], n, 0, PASSES)
 
         firsts = [
-            keep.tile([P, 1, N_SMALL, 4], BF16, name="grouped00", align_bytes=64),
-            after.tile([P, 1, N_SMALL, 4], BF16, name="grouped01", offset=1536, align_bytes=64),
+            keep.tile([P, 1, N, 4], BF16, name="grouped00", align_bytes=64),
+            late.tile([P, 1, N, 4], BF16, name="grouped01", offset=4032, align_bytes=64),
         ]
         for a in range(PASSES):
             interleave(nc.vector.tensor_copy, firsts[a][:, 0], raw[0][a][:])
             quantize(firsts[a][:], 0, a, a + 1)
-        wins.append(after.tile([P, T], F32, name="win_last", offset=2048, align_bytes=64))
-        nc.vector.memset(wins[-1][:].bitcast(I32), 0)
-        raw.append([load_x(1, 0, offset=1024), load_x(1, 1, offset=4096)])
-        wgo_sb = keep.tile([P, S], F32, name="wgo_sb", tag="raw0", align_bytes=64)
-        nc.sync.dma_start(out=wgo_sb[:], in_=wgo)
-        words_late = []
 
-        def product(c, j0, j1, val):
+        def late_window(offset):
+            win = late.tile([P, T], F32, name=f"win{len(wins)}", offset=offset, align_bytes=64)
+            nc.gpsimd.memset(win[:].bitcast(I32), 0)
+            wins.append(win)
+
+        def place(c, j0, j1, pool=keep, offset=None):
+            val = pool.tile([P, j1 - j0], F32, name=f"val{c}_{j0}", offset=offset, align_bytes=64)
             acc = psum.tile([P, S], F32, name="acc")
-            step = N_SMALL
-            words, first = (words_early, 0) if c < EARLY_TILES else (words_late[0], EARLY_TILES)
-            w0 = (c - first) * P // 2
-            for m0 in range(j0, j1, step):
-                for a in range(PASSES):
-                    nc.tensor.matmul_mx(
-                        out=acc[:, m0 - j0 : m0 - j0 + step],
-                        lhsT=words[:, a, w0 : w0 + P // 2].bitcast(U8).bitcast(FP4X4),
-                        lhsT_scale=planes[:, a, P * c : P * (c + 1)],
-                        rhs=codes[:, m0 // step, a, :].bitcast(FP8X4),
-                        rhs_scale=scales[:, m0 // step, a, :],
-                        start=(a == 0),
-                        stop=(a == PASSES - 1),
-                    )
-            nc.scalar.activation(out=val, in_=acc[:, 0 : j1 - j0], func=GELU, bias=bias[:, c : c + 1])
-
-        def place(c, j0, j1, val=None):
-            if val is None:
-                fresh = vals.tile([P, S], F32, name="val")
-                val = fresh[:, 0 : j1 - j0]
-            product(c, j0, j1, val)
+            for n, (p0, p1) in enumerate(PIECES):
+                for m0 in range(max(j0, p0), min(j1, p1), N):
+                    for a in range(PASSES):
+                        nc.tensor.matmul_mx(
+                            out=acc[:, m0 - j0 : m0 - j0 + N],
+                            lhsT=words[c][:, a].bitcast(U8).bitcast(FP4X4),
+                            lhsT_scale=planes[:, a, P * c : P * (c + 1)],
+                            rhs=codes[n][:, a, m0 - p0 : m0 - p0 + N].bitcast(FP8X4),
+                            rhs_scale=scales[n][:, a, m0 - p0 : m0 - p0 + N],
+                            start=(a == 0),
+                            stop=(a == PASSES - 1),
+                        )
+            nc.scalar.activation(out=val[:], in_=acc[:, 0 : j1 - j0], func=GELU, bias=bias[:, c : c + 1])
             win = wins[c % WINDOWS]
-            weights = wgo_first[:] if j1 == PIECES[0][1] else wgo_sb[:, j0:j1]
-            nc.vector.tensor_tensor(win[:].indirect(offsets[:, j0 // 16 : j1 // 16]), val, weights, MULT)
+            nc.vector.tensor_tensor(win[:].indirect(offsets[:, j0 // 16 : j1 // 16]), val[:], weights[:, j0:j1], MULT)
             if j1 == S:
                 rows = out[P * c : P * (c + 1), :]
                 if c < TILES - 1:
@@ -154,29 +148,22 @@ def tile_list_hscat_gelu_kernel(tc, x, w_words, w_scales, b, wgo, offs, out):
                     for queue, t0 in ((nc.sync, 0), (nc.scalar, T // 2)):
                         queue.dma_start(out=rows[:, t0 : t0 + T // 2], in_=win[:, t0 : t0 + T // 2])
 
-        def held(name, offset, width):
-            val = slide.tile([P, width], F32, name=name, offset=offset, align_bytes=64)
-            return val[:]
-
-        place(0, 0, 128)
-        place(1, 0, 128)
-        quantize_later(1)
-        raw.append([load_x(2, 0, offset=0, pool=after), load_x(2, 1, offset=2048)])
-        raw.append([load_x(3, 0, offset=6144), load_x(3, 1, offset=8192)])
-        place(2, 0, 128, held("val20", 4096, 128))
-        place(3, 0, 128, held("val30", 4608, 128))
-        place(0, 128, 256)
-        place(1, 128, 256)
-        quantize_later(2)
-        place(2, 128, 256, held("val21", 2048, 128))
-        place(3, 128, 256, held("val31", 2560, 128))
-        quantize_later(3)
-        words_late.append(load_words(EARLY_TILES, TILES, "grouped3"))
-        place(0, 256, 384, held("val02", 8192, 128))
-        place(1, 256, 384, held("val12", 8704, 128))
-        for c in (0, 1):
-            place(c, 384, S)
-        for c in (2, 3):
+        late_window(0)
+        late_window(4992)
+        place(0, 0, 128, late, 9088)
+        late_window(9088)
+        grouped1 = late.tile([P, PASSES, N, 4], BF16, name="grouped1", offset=13184, align_bytes=64)
+        for c in (1, 2, 3):
+            place(c, 0, 128)
+        quantize_later(1, grouped1)
+        place(4, 0, 128, held, 6144)
+        place(5, 0, 128, held, 6656)
+        for c in range(4):
+            place(c, 128, 256)
+        quantize_later(2, keep.tile([P, PASSES, 2 * N, 4], BF16, name="grouped2", align_bytes=64))
+        place(4, 128, 256, held, 12288)
+        place(5, 128, 256, held, 12800)
+        for c in range(WINDOWS):
             place(c, 256, S)
-        for c in range(EARLY_TILES, TILES):
+        for c in range(WINDOWS, TILES):
             place(c, 0, S)

@@ -21,7 +21,7 @@ PASSES = K // 512
 TILES = M // P
 N = 128
 PIECES = [(0, 128), (128, 256), (256, 512)]
-WORD_LOADS = [(0, 4), (4, 6), (6, 8)]
+WORD_LOADS = [(0, 2), (2, 4), (4, 6), (6, 8)]
 WINDOWS = 6
 
 
@@ -48,7 +48,6 @@ def tile_list_hscat_gelu_kernel(tc, x, w_words, w_scales, b, wgo, offs, out):
         warm = keep.tile([P, 1], F32, name="warm")
         b_rows = keep.tile([P, P], F32, name="b_rows", align_bytes=64)
         b_turned = keep.tile([P, P], F32, name="b_turned", align_bytes=64)
-        bias = keep.tile([P, TILES], F32, name="bias")
         weights = keep.tile([P, S], F32, name="weights", align_bytes=64)
 
         x_view = x.rearrange("(a p i) j -> a p i j", a=PASSES, i=4)
@@ -75,24 +74,22 @@ def tile_list_hscat_gelu_kernel(tc, x, w_words, w_scales, b, wgo, offs, out):
             nc.sync.dma_start(out=weights[:, j0:j1], in_=wgo[:, j0:j1])
 
         nc.gpsimd.memset(planes_i32, 0)
+        raw = [[load_x(0, 0, 0), load_x(0, 1, 2048)]]
         nc.sync.dma_start(
             out=b_rows[:], in_=b.rearrange("(c p) -> c p", p=P).unsqueeze(0).to_broadcast([P // TILES, TILES, P])
         )
-        raw = [[load_x(0, 0, 0), load_x(0, 1, 2048)]]
         for q in range(4):
             nc.sync.dma_start(out=planes_i32_3[32 * q : 32 * q + 4], in_=s_view[4 * q : 4 * q + 4])
         load_words(*WORD_LOADS[0])
-        nc.sync.dma_start(offsets[:], offs)
         load_weights(0, N)
-        raw.append([load_x(1, 0, 4096), load_x(1, 1, 6144)])
+        nc.sync.dma_start(offsets[:], offs)
         load_words(*WORD_LOADS[1])
+        raw.append([load_x(1, 0, 4096), load_x(1, 1, 6144)])
+        load_words(*WORD_LOADS[2])
         load_weights(N, S)
         raw.append([load_x(2, 0, 8192), load_x(2, 1, 12288)])
-        load_words(*WORD_LOADS[2])
+        load_words(*WORD_LOADS[3])
 
-        nc.vector.transpose(b_turned[:], b_rows[:])
-        for u in range(4):
-            nc.scalar.copy(out=bias[32 * u : 32 * u + 32, :], in_=b_turned[32 * u : 32 * u + 32, 32 * u : 32 * u + TILES])
         for win in wins:
             nc.vector.memset(win[:].bitcast(I32), 0)
         nc.scalar.activation(out=warm[:], in_=wins[0][:, 0:1], func=GELU)
@@ -115,7 +112,12 @@ def tile_list_hscat_gelu_kernel(tc, x, w_words, w_scales, b, wgo, offs, out):
         ]
         for a in range(PASSES):
             interleave(nc.vector.tensor_copy, firsts[a][:, 0], raw[0][a][:])
+            if a == PASSES - 1:
+                nc.vector.transpose(b_turned[:], b_rows[:])
             quantize(firsts[a][:], 0, a, a + 1)
+        for u in range(1, 4):
+            rows = slice(32 * u, 32 * u + 32)
+            nc.scalar.copy(out=b_turned[rows, 0:TILES], in_=b_turned[rows, 32 * u : 32 * u + TILES])
 
         def late_window(offset):
             win = late.tile([P, T], F32, name=f"win{len(wins)}", offset=offset, align_bytes=64)
@@ -137,16 +139,11 @@ def tile_list_hscat_gelu_kernel(tc, x, w_words, w_scales, b, wgo, offs, out):
                             start=(a == 0),
                             stop=(a == PASSES - 1),
                         )
-            nc.scalar.activation(out=val[:], in_=acc[:, 0 : j1 - j0], func=GELU, bias=bias[:, c : c + 1])
+            nc.scalar.activation(out=val[:], in_=acc[:, 0 : j1 - j0], func=GELU, bias=b_turned[:, c : c + 1])
             win = wins[c % WINDOWS]
             nc.vector.tensor_tensor(win[:].indirect(offsets[:, j0 // 16 : j1 // 16]), val[:], weights[:, j0:j1], MULT)
             if j1 == S:
-                rows = out[P * c : P * (c + 1), :]
-                if c < TILES - 1:
-                    nc.sync.dma_start(out=rows, in_=win[:])
-                else:
-                    for queue, t0 in ((nc.sync, 0), (nc.scalar, T // 2)):
-                        queue.dma_start(out=rows[:, t0 : t0 + T // 2], in_=win[:, t0 : t0 + T // 2])
+                nc.sync.dma_start(out=out[P * c : P * (c + 1), :], in_=win[:])
 
         late_window(0)
         late_window(4992)

@@ -23,6 +23,7 @@ N = 128
 PIECES = [(0, 128), (128, 256), (256, 512)]
 WORD_LOADS = [(0, 2), (2, 4), (4, 6), (6, 8)]
 WINDOWS = 6
+HALF = M // 2
 
 
 def interleave(copy, dst, src):
@@ -41,7 +42,7 @@ def tile_list_hscat_gelu_kernel(tc, x, w_words, w_scales, b, wgo, offs, out):
         held = ctx.enter_context(tc.tile_pool(name="held", bufs=1))
 
         offsets = keep.tile([P, S // 16], U16, name="offsets")
-        planes = keep.tile([P, PASSES, M], U8, name="planes", align_bytes=64)
+        planes = [keep.tile([P, PASSES, HALF], U8, name=f"planes{h}", align_bytes=64) for h in range(2)]
         codes = [keep.tile([P, PASSES, j1 - j0], U32, name=f"codes{j0}", align_bytes=64) for j0, j1 in PIECES]
         scales = [keep.tile([P, PASSES, j1 - j0], U8, name=f"scales{j0}", align_bytes=64) for j0, j1 in PIECES]
         wins = [keep.tile([P, T], F32, name=f"win{w}") for w in range(3)]
@@ -53,8 +54,14 @@ def tile_list_hscat_gelu_kernel(tc, x, w_words, w_scales, b, wgo, offs, out):
         x_view = x.rearrange("(a p i) j -> a p i j", a=PASSES, i=4)
         w_view = w_words.bitcast(I32).rearrange("a p n -> p a n")
         s_view = w_scales.bitcast(I32).rearrange("a q n -> q a n")
-        planes_i32 = planes[:].rearrange("p a n -> p (a n)").bitcast(I32)
-        planes_i32_3 = planes_i32.rearrange("p (a n) -> p a n", a=PASSES)
+        planes_i32 = [half[:].rearrange("p a n -> p (a n)").bitcast(I32) for half in planes]
+
+        def load_scales(h):
+            rows = planes_i32[h].rearrange("p (a n) -> p a n", a=PASSES)
+            for q in (0, 2, 1, 3):
+                nc.sync.dma_start(
+                    out=rows[32 * q : 32 * q + 4], in_=s_view[4 * q : 4 * q + 4, :, h * HALF // 4 : (h + 1) * HALF // 4]
+                )
 
         def load_x(n, a, offset):
             j0, j1 = PIECES[n]
@@ -73,19 +80,20 @@ def tile_list_hscat_gelu_kernel(tc, x, w_words, w_scales, b, wgo, offs, out):
         def load_weights(j0, j1):
             nc.sync.dma_start(out=weights[:, j0:j1], in_=wgo[:, j0:j1])
 
-        nc.gpsimd.memset(planes_i32, 0)
+        for half in planes_i32:
+            nc.gpsimd.memset(half, 0)
         raw = [[load_x(0, 0, 0), load_x(0, 1, 2048)]]
         nc.sync.dma_start(
             out=b_rows[:], in_=b.rearrange("(c p) -> c p", p=P).unsqueeze(0).to_broadcast([P // TILES, TILES, P])
         )
-        for q in range(4):
-            nc.sync.dma_start(out=planes_i32_3[32 * q : 32 * q + 4], in_=s_view[4 * q : 4 * q + 4])
+        load_scales(0)
         load_words(*WORD_LOADS[0])
         load_weights(0, N)
         nc.sync.dma_start(offsets[:], offs)
         load_words(*WORD_LOADS[1])
         raw.append([load_x(1, 0, 4096), load_x(1, 1, 6144)])
         load_words(*WORD_LOADS[2])
+        load_scales(1)
         load_weights(N, S)
         raw.append([load_x(2, 0, 8192), load_x(2, 1, 12288)])
         load_words(*WORD_LOADS[3])
@@ -133,7 +141,7 @@ def tile_list_hscat_gelu_kernel(tc, x, w_words, w_scales, b, wgo, offs, out):
                         nc.tensor.matmul_mx(
                             out=acc[:, m0 - j0 : m0 - j0 + N],
                             lhsT=words[c][:, a].bitcast(U8).bitcast(FP4X4),
-                            lhsT_scale=planes[:, a, P * c : P * (c + 1)],
+                            lhsT_scale=planes[c // 4][:, a, P * (c % 4) : P * (c % 4 + 1)],
                             rhs=codes[n][:, a, m0 - p0 : m0 - p0 + N].bitcast(FP8X4),
                             rhs_scale=scales[n][:, a, m0 - p0 : m0 - p0 + N],
                             start=(a == 0),

@@ -22,7 +22,7 @@ TILES = M // P
 N = 128
 PIECES = [(0, 128), (128, 256), (256, 512)]
 WORD_LOADS = [(0, 2), (2, 4), (4, 6), (6, 8)]
-WINDOWS = 6
+WINDOWS = 5
 HALF = M // 2
 
 
@@ -45,7 +45,7 @@ def tile_list_hscat_gelu_kernel(tc, x, w_words, w_scales, b, wgo, offs, out):
         planes = [keep.tile([P, PASSES, HALF], U8, name=f"planes{h}", align_bytes=64) for h in range(2)]
         codes = [keep.tile([P, PASSES, j1 - j0], U32, name=f"codes{j0}", align_bytes=64) for j0, j1 in PIECES]
         scales = [keep.tile([P, PASSES, j1 - j0], U8, name=f"scales{j0}", align_bytes=64) for j0, j1 in PIECES]
-        wins = [keep.tile([P, T], F32, name=f"win{w}") for w in range(3)]
+        wins = [keep.tile([P, T], F32, name=f"win{w}") for w in range(2)]
         warm = keep.tile([P, 1], F32, name="warm")
         b_rows = keep.tile([P, P], F32, name="b_rows", align_bytes=64)
         b_turned = keep.tile([P, P], F32, name="b_turned", align_bytes=64)
@@ -158,16 +158,16 @@ def tile_list_hscat_gelu_kernel(tc, x, w_words, w_scales, b, wgo, offs, out):
         place(0, 0, 128, late, 9088)
         late_window(9088)
         grouped1 = late.tile([P, PASSES, N, 4], BF16, name="grouped1", offset=13184, align_bytes=64)
-        for c in (1, 2, 3):
+        for c in (1, 2):
             place(c, 0, 128)
         quantize_later(1, grouped1)
-        place(4, 0, 128, held, 6144)
-        place(5, 0, 128, held, 6656)
-        for c in range(4):
+        place(3, 0, 128, held, 6144)
+        place(4, 0, 128, held, 6656)
+        for c in range(3):
             place(c, 128, 256)
         quantize_later(2, keep.tile([P, PASSES, 2 * N, 4], BF16, name="grouped2", align_bytes=64))
-        place(4, 128, 256, held, 12288)
-        place(5, 128, 256, held, 12800)
+        place(3, 128, 256, held, 12288)
+        place(4, 128, 256, held, 12800)
         for c in range(WINDOWS):
             place(c, 256, S)
         for c in range(WINDOWS, TILES):

@@ -48,7 +48,7 @@ def tile_list_hscat_gelu_kernel(tc, x, w_words, w_scales, b, wgo, offs, out):
         wins = [keep.tile([P, T], F32, name=f"win{w}") for w in range(2)]
         warm = keep.tile([P, 1], F32, name="warm")
         b_rows = keep.tile([P, P], F32, name="b_rows", align_bytes=64)
-        b_turned = keep.tile([P, P], F32, name="b_turned", align_bytes=64)
+        b_turned = keep.tile([P, 32], F32, name="b_turned", align_bytes=64)
         weights = keep.tile([P, S], F32, name="weights", align_bytes=64)
 
         x_view = x.rearrange("(a p i) j -> a p i j", a=PASSES, i=4)
@@ -120,12 +120,11 @@ def tile_list_hscat_gelu_kernel(tc, x, w_words, w_scales, b, wgo, offs, out):
         ]
         for a in range(PASSES):
             interleave(nc.vector.tensor_copy, firsts[a][:, 0], raw[0][a][:])
-            if a == PASSES - 1:
-                nc.vector.transpose(b_turned[:], b_rows[:])
             quantize(firsts[a][:], 0, a, a + 1)
         for u in range(1, 4):
             rows = slice(32 * u, 32 * u + 32)
-            nc.scalar.copy(out=b_turned[rows, 0:TILES], in_=b_turned[rows, 32 * u : 32 * u + TILES])
+            nc.scalar.copy(out=b_rows[rows, 0:32], in_=b_rows[rows, 32 * u : 32 * u + 32])
+        nc.vector.transpose(b_turned[:], b_rows[:, 0:32])
 
         def late_window(offset):
             win = late.tile([P, T], F32, name=f"win{len(wins)}", offset=offset, align_bytes=64)
@@ -161,7 +160,7 @@ def tile_list_hscat_gelu_kernel(tc, x, w_words, w_scales, b, wgo, offs, out):
         for c in (1, 2):
             place(c, 0, 128)
         quantize_later(1, grouped1)
-        place(3, 0, 128, held, 6144)
+        place(3, 0, 128, held, 4096)
         place(4, 0, 128, held, 6656)
         for c in range(3):
             place(c, 128, 256)

@@ -21,7 +21,6 @@ PASSES = K // 512
 TILES = M // P
 N = 128
 PIECES = [(0, 128), (128, 256), (256, 512)]
-WORD_LOADS = [(0, 2), (2, 4), (4, 6), (6, 8)]
 WINDOWS = 5
 HALF = M // 2
 
@@ -47,8 +46,7 @@ def tile_list_hscat_gelu_kernel(tc, x, w_words, w_scales, b, wgo, offs, out):
         scales = [keep.tile([P, PASSES, j1 - j0], U8, name=f"scales{j0}", align_bytes=64) for j0, j1 in PIECES]
         wins = [keep.tile([P, T], F32, name=f"win{w}") for w in range(2)]
         warm = keep.tile([P, 1], F32, name="warm")
-        b_rows = keep.tile([P, P], F32, name="b_rows", align_bytes=64)
-        b_turned = keep.tile([P, 32], F32, name="b_turned", align_bytes=64)
+        b_rows = keep.tile([P, 32], F32, name="b_rows", align_bytes=64)
         weights = keep.tile([P, S], F32, name="weights", align_bytes=64)
 
         x_view = x.rearrange("(a p i) j -> a p i j", a=PASSES, i=4)
@@ -71,35 +69,33 @@ def tile_list_hscat_gelu_kernel(tc, x, w_words, w_scales, b, wgo, offs, out):
 
         words = {}
 
-        def load_words(c0, c1):
-            tile = keep.tile([P, PASSES, (c1 - c0) * P // 2], I32, name=f"words{c0}", align_bytes=64)
-            nc.sync.dma_start(out=tile[:], in_=w_view[:, :, c0 * P // 2 : c1 * P // 2])
-            for c in range(c0, c1):
+        def load_words(c0):
+            tile = keep.tile([P, PASSES, P], I32, name=f"words{c0}", align_bytes=64)
+            nc.sync.dma_start(out=tile[:], in_=w_view[:, :, c0 * P // 2 : (c0 + 2) * P // 2])
+            for c in (c0, c0 + 1):
                 words[c] = tile[:, :, (c - c0) * P // 2 : (c - c0 + 1) * P // 2]
 
         def load_weights(j0, j1):
             nc.sync.dma_start(out=weights[:, j0:j1], in_=wgo[:, j0:j1])
 
-        for half in planes_i32:
-            nc.gpsimd.memset(half, 0)
-        raw = [[load_x(0, 0, 0), load_x(0, 1, 2048)]]
-        nc.sync.dma_start(
-            out=b_rows[:], in_=b.rearrange("(c p) -> c p", p=P).unsqueeze(0).to_broadcast([P // TILES, TILES, P])
-        )
+        nc.vector.memset(b_rows[:], 0.0)
+        raw = [[load_x(0, 0, 0)]]
+        nc.sync.dma_start(out=b_rows[0:P:4, :], in_=b.rearrange("(c q j) -> q c j", c=TILES, q=4))
+        raw[0].append(load_x(0, 1, 2048))
         load_scales(0)
-        load_words(*WORD_LOADS[0])
+        load_words(0)
         load_weights(0, N)
         nc.sync.dma_start(offsets[:], offs)
-        load_words(*WORD_LOADS[1])
+        for win in wins:
+            nc.vector.memset(win[:].bitcast(I32), 0)
+        load_words(2)
         raw.append([load_x(1, 0, 4096), load_x(1, 1, 6144)])
-        load_words(*WORD_LOADS[2])
+        load_words(4)
         load_scales(1)
         load_weights(N, S)
         raw.append([load_x(2, 0, 8192), load_x(2, 1, 12288)])
-        load_words(*WORD_LOADS[3])
+        load_words(6)
 
-        for win in wins:
-            nc.vector.memset(win[:].bitcast(I32), 0)
         nc.scalar.activation(out=warm[:], in_=wins[0][:, 0:1], func=GELU)
 
         def quantize(grouped, n, a0, a1):
@@ -118,13 +114,12 @@ def tile_list_hscat_gelu_kernel(tc, x, w_words, w_scales, b, wgo, offs, out):
             keep.tile([P, 1, N, 4], BF16, name="grouped00", align_bytes=64),
             late.tile([P, 1, N, 4], BF16, name="grouped01", offset=4032, align_bytes=64),
         ]
-        for a in range(PASSES):
-            interleave(nc.vector.tensor_copy, firsts[a][:, 0], raw[0][a][:])
-            quantize(firsts[a][:], 0, a, a + 1)
-        for u in range(1, 4):
-            rows = slice(32 * u, 32 * u + 32)
-            nc.scalar.copy(out=b_rows[rows, 0:32], in_=b_rows[rows, 32 * u : 32 * u + 32])
-        nc.vector.transpose(b_turned[:], b_rows[:, 0:32])
+        interleave(nc.vector.tensor_copy, firsts[0][:, 0], raw[0][0][:])
+        b_turned = keep.tile([P, 32], F32, name="b_turned", align_bytes=64)
+        nc.vector.transpose(b_turned[:], b_rows[:])
+        quantize(firsts[0][:], 0, 0, 1)
+        interleave(nc.vector.tensor_copy, firsts[1][:, 0], raw[0][1][:])
+        quantize(firsts[1][:], 0, 1, 2)
 
         def late_window(offset):
             win = late.tile([P, T], F32, name=f"win{len(wins)}", offset=offset, align_bytes=64)
@@ -146,7 +141,7 @@ def tile_list_hscat_gelu_kernel(tc, x, w_words, w_scales, b, wgo, offs, out):
                             start=(a == 0),
                             stop=(a == PASSES - 1),
                         )
-            nc.scalar.activation(out=val[:], in_=acc[:, 0 : j1 - j0], func=GELU, bias=b_turned[:, c : c + 1])
+            nc.scalar.activation(out=val[:], in_=acc[:, 0 : j1 - j0], func=GELU, bias=b_turned[:, 4 * c : 4 * c + 1])
             win = wins[c % WINDOWS]
             nc.vector.tensor_tensor(win[:].indirect(offsets[:, j0 // 16 : j1 // 16]), val[:], weights[:, j0:j1], MULT)
             if j1 == S:

@@ -44,7 +44,7 @@ def tile_list_hscat_gelu_kernel(tc, x, w_words, w_scales, b, wgo, offs, out):
         planes = [keep.tile([P, PASSES, HALF], U8, name=f"planes{h}", align_bytes=64) for h in range(2)]
         codes = [keep.tile([P, PASSES, j1 - j0], U32, name=f"codes{j0}", align_bytes=64) for j0, j1 in PIECES]
         scales = [keep.tile([P, PASSES, j1 - j0], U8, name=f"scales{j0}", align_bytes=64) for j0, j1 in PIECES]
-        wins = [keep.tile([P, T], F32, name=f"win{w}") for w in range(2)]
+        wins = [keep.tile([P, T], F32, name=f"win{w}") for w in range(3)]
         warm = keep.tile([P, 1], F32, name="warm")
         b_rows = keep.tile([P, 32], F32, name="b_rows", align_bytes=64)
         weights = keep.tile([P, S], F32, name="weights", align_bytes=64)
@@ -149,12 +149,9 @@ def tile_list_hscat_gelu_kernel(tc, x, w_words, w_scales, b, wgo, offs, out):
 
         late_window(0)
         late_window(4992)
-        place(0, 0, 128, late, 9088)
-        late_window(9088)
-        grouped1 = late.tile([P, PASSES, N, 4], BF16, name="grouped1", offset=13184, align_bytes=64)
-        for c in (1, 2):
+        for c in range(3):
             place(c, 0, 128)
-        quantize_later(1, grouped1)
+        quantize_later(1, keep.tile([P, PASSES, N, 4], BF16, name="grouped1", align_bytes=64))
         place(3, 0, 128, held, 4096)
         place(4, 0, 128, held, 6656)
         for c in range(3):

@@ -21,7 +21,7 @@ PASSES = K // 512
 TILES = M // P
 N = 128
 PIECES = [(0, 128), (128, 256), (256, 512)]
-WINDOWS = 5
+WINDOWS = 8
 HALF = M // 2
 
 
@@ -92,9 +92,10 @@ def tile_list_hscat_gelu_kernel(tc, x, w_words, w_scales, b, wgo, offs, out):
         raw.append([load_x(1, 0, 4096), load_x(1, 1, 6144)])
         load_words(4)
         load_scales(1)
-        load_weights(N, S)
-        raw.append([load_x(2, 0, 8192), load_x(2, 1, 12288)])
+        load_weights(N, 2 * N)
         load_words(6)
+        raw.append([load_x(2, 0, 8192), load_x(2, 1, 12288)])
+        load_weights(2 * N, S)
 
         nc.scalar.activation(out=warm[:], in_=wins[0][:, 0:1], func=GELU)
 
@@ -130,14 +131,14 @@ def tile_list_hscat_gelu_kernel(tc, x, w_words, w_scales, b, wgo, offs, out):
             val = pool.tile([P, j1 - j0], F32, name=f"val{c}_{j0}", offset=offset, align_bytes=64)
             acc = psum.tile([P, S], F32, name="acc")
             for n, (p0, p1) in enumerate(PIECES):
-                for m0 in range(max(j0, p0), min(j1, p1), N):
+                if j0 <= p0 and p1 <= j1:
                     for a in range(PASSES):
                         nc.tensor.matmul_mx(
-                            out=acc[:, m0 - j0 : m0 - j0 + N],
+                            out=acc[:, p0 - j0 : p1 - j0],
                             lhsT=words[c][:, a].bitcast(U8).bitcast(FP4X4),
                             lhsT_scale=planes[c // 4][:, a, P * (c % 4) : P * (c % 4 + 1)],
-                            rhs=codes[n][:, a, m0 - p0 : m0 - p0 + N].bitcast(FP8X4),
-                            rhs_scale=scales[n][:, a, m0 - p0 : m0 - p0 + N],
+                            rhs=codes[n][:, a].bitcast(FP8X4),
+                            rhs_scale=scales[n][:, a],
                             start=(a == 0),
                             stop=(a == PASSES - 1),
                         )
@@ -149,17 +150,21 @@ def tile_list_hscat_gelu_kernel(tc, x, w_words, w_scales, b, wgo, offs, out):
 
         late_window(0)
         late_window(4992)
-        for c in range(3):
+        place(0, 0, 128, late, 9088)
+        late_window(9088)
+        for c in (1, 2):
             place(c, 0, 128)
-        quantize_later(1, keep.tile([P, PASSES, N, 4], BF16, name="grouped1", align_bytes=64))
+        quantize_later(1, late.tile([P, PASSES, N, 4], BF16, name="grouped1", offset=17216, align_bytes=64))
+        late_window(13184)
+        late_window(19200)
         place(3, 0, 128, held, 4096)
         place(4, 0, 128, held, 6656)
-        for c in range(3):
-            place(c, 128, 256)
+        place(5, 0, 256)
+        place(6, 0, 256)
         quantize_later(2, keep.tile([P, PASSES, 2 * N, 4], BF16, name="grouped2", align_bytes=64))
-        place(3, 128, 256, held, 12288)
-        place(4, 128, 256, held, 12800)
-        for c in range(WINDOWS):
+        place(7, 0, 256, held, 12288)
+        place(5, 256, S)
+        for c in range(5):
+            place(c, 128, S)
+        for c in (6, 7):
             place(c, 256, S)
-        for c in range(WINDOWS, TILES):
-            place(c, 0, S)

@@ -84,11 +84,11 @@ def tile_list_hscat_gelu_kernel(tc, x, w_words, w_scales, b, wgo, offs, out):
         raw[0].append(load_x(0, 1, 2048))
         load_scales(0)
         load_words(0)
+        load_words(2)
         load_weights(0, N)
         nc.sync.dma_start(offsets[:], offs)
         for win in wins:
             nc.vector.memset(win[:].bitcast(I32), 0)
-        load_words(2)
         raw.append([load_x(1, 0, 4096), load_x(1, 1, 6144)])
         load_words(4)
         load_scales(1)

@@ -122,9 +122,9 @@ def tile_list_hscat_gelu_kernel(tc, x, w_words, w_scales, b, wgo, offs, out):
         interleave(nc.vector.tensor_copy, firsts[1][:, 0], raw[0][1][:])
         quantize(firsts[1][:], 0, 1, 2)
 
-        def late_window(offset):
-            win = late.tile([P, T], F32, name=f"win{len(wins)}", offset=offset, align_bytes=64)
-            nc.gpsimd.memset(win[:].bitcast(I32), 0)
+        def late_window(offset, engine=nc.gpsimd, pool=late):
+            win = pool.tile([P, T], F32, name=f"win{len(wins)}", offset=offset, align_bytes=64)
+            engine.memset(win[:].bitcast(I32), 0)
             wins.append(win)
 
         def place(c, j0, j1, pool=keep, offset=None):
@@ -148,17 +148,17 @@ def tile_list_hscat_gelu_kernel(tc, x, w_words, w_scales, b, wgo, offs, out):
             if j1 == S:
                 nc.sync.dma_start(out=out[P * c : P * (c + 1), :], in_=win[:])
 
-        late_window(0)
-        late_window(4992)
-        place(0, 0, 128, late, 9088)
-        late_window(9088)
+        late_window(0, nc.vector)
+        place(0, 0, 128, late, 5056)
+        late_window(5056)
         for c in (1, 2):
             place(c, 0, 128)
-        quantize_later(1, late.tile([P, PASSES, N, 4], BF16, name="grouped1", offset=17216, align_bytes=64))
-        late_window(13184)
-        late_window(19200)
+        quantize_later(1, late.tile([P, PASSES, N, 4], BF16, name="grouped1", offset=13184, align_bytes=64))
+        late_window(9152)
+        late_window(15168)
         place(3, 0, 128, held, 4096)
         place(4, 0, 128, held, 6656)
+        late_window(3072, pool=held)
         place(5, 0, 256)
         place(6, 0, 256)
         quantize_later(2, keep.tile([P, PASSES, 2 * N, 4], BF16, name="grouped2", align_bytes=64))

@@ -42,8 +42,8 @@ def tile_list_hscat_gelu_kernel(tc, x, w_words, w_scales, b, wgo, offs, out):
 
         offsets = keep.tile([P, S // 16], U16, name="offsets")
         planes = [keep.tile([P, PASSES, HALF], U8, name=f"planes{h}", align_bytes=64) for h in range(2)]
-        codes = [keep.tile([P, PASSES, j1 - j0], U32, name=f"codes{j0}", align_bytes=64) for j0, j1 in PIECES]
-        scales = [keep.tile([P, PASSES, j1 - j0], U8, name=f"scales{j0}", align_bytes=64) for j0, j1 in PIECES]
+        codes = [keep.tile([P, PASSES, N], U32, name=f"codes{g}", align_bytes=64) for g in range(S // N)]
+        scales = [keep.tile([P, PASSES, N], U8, name=f"scales{g}", align_bytes=64) for g in range(S // N)]
         wins = [keep.tile([P, T], F32, name=f"win{w}") for w in range(3)]
         warm = keep.tile([P, 1], F32, name="warm")
         b_rows = keep.tile([P, 32], F32, name="b_rows", align_bytes=64)
@@ -127,43 +127,52 @@ def tile_list_hscat_gelu_kernel(tc, x, w_words, w_scales, b, wgo, offs, out):
             engine.memset(win[:].bitcast(I32), 0)
             wins.append(win)
 
-        def place(c, j0, j1, pool=keep, offset=None):
+        def place(c, j0, j1, pool=keep, offset=None, sums=None):
             val = pool.tile([P, j1 - j0], F32, name=f"val{c}_{j0}", offset=offset, align_bytes=64)
-            acc = psum.tile([P, S], F32, name="acc")
-            for n, (p0, p1) in enumerate(PIECES):
-                if j0 <= p0 and p1 <= j1:
-                    for a in range(PASSES):
-                        nc.tensor.matmul_mx(
-                            out=acc[:, p0 - j0 : p1 - j0],
-                            lhsT=words[c][:, a].bitcast(U8).bitcast(FP4X4),
-                            lhsT_scale=planes[c // 4][:, a, P * (c % 4) : P * (c % 4 + 1)],
-                            rhs=codes[n][:, a].bitcast(FP8X4),
-                            rhs_scale=scales[n][:, a],
-                            start=(a == 0),
-                            stop=(a == PASSES - 1),
-                        )
-            nc.scalar.activation(out=val[:], in_=acc[:, 0 : j1 - j0], func=GELU, bias=b_turned[:, 4 * c : 4 * c + 1])
+            for g0, g1 in sums or [(j0 // N, j1 // N)]:
+                multiply(c, g0, g1, val[:, g0 * N - j0 : g1 * N - j0])
             win = wins[c % WINDOWS]
             nc.vector.tensor_tensor(win[:].indirect(offsets[:, j0 // 16 : j1 // 16]), val[:], weights[:, j0:j1], MULT)
             if j1 == S:
                 nc.sync.dma_start(out=out[P * c : P * (c + 1), :], in_=win[:])
 
-        late_window(0, nc.vector)
-        place(0, 0, 128, late, 5056)
-        late_window(5056)
-        for c in (1, 2):
+        def multiply(c, g0, g1, val):
+            acc = psum.tile([P, S], F32, name="acc")
+            for g in sorted(range(g0, g1), key=lambda g: g == 2):
+                for a in range(PASSES):
+                    nc.tensor.matmul_mx(
+                        out=acc[:, (g - g0) * N : (g - g0 + 1) * N],
+                        lhsT=words[c][:, a].bitcast(U8).bitcast(FP4X4),
+                        lhsT_scale=planes[c // 4][:, a, P * (c % 4) : P * (c % 4 + 1)],
+                        rhs=codes[g][:, a].bitcast(FP8X4),
+                        rhs_scale=scales[g][:, a],
+                        start=(a == 0),
+                        stop=(a == PASSES - 1),
+                    )
+            nc.scalar.activation(out=val, in_=acc[:, 0 : (g1 - g0) * N], func=GELU, bias=b_turned[:, 4 * c : 4 * c + 1])
+
+        late_window(0, nc.vector, held)
+        late_window(0)
+        late_window(4992)
+        for c in range(3):
             place(c, 0, 128)
-        quantize_later(1, late.tile([P, PASSES, N, 4], BF16, name="grouped1", offset=13184, align_bytes=64))
-        late_window(9152)
-        late_window(15168)
+        quantize_later(1, late.tile([P, PASSES, N, 4], BF16, name="grouped1", offset=13120, align_bytes=64))
+        late_window(9088)
+        late_window(15104)
         place(3, 0, 128, held, 4096)
         place(4, 0, 128, held, 6656)
-        late_window(3072, pool=held)
         place(5, 0, 256)
         place(6, 0, 256)
-        quantize_later(2, keep.tile([P, PASSES, 2 * N, 4], BF16, name="grouped2", align_bytes=64))
+        grouped2 = keep.tile([P, 2, PASSES, N, 4], BF16, name="grouped2", align_bytes=64)
+        for a in range(PASSES):
+            nc.scalar.copy(
+                out=grouped2[:, :, a].rearrange("p h (c i) t -> p h c t i", i=4),
+                in_=raw[2][a][:].rearrange("p t (h c i) -> p h c t i", h=2, i=4),
+            )
+        for h in range(2):
+            quantize(grouped2[:, h], 2 + h, 0, PASSES)
         place(7, 0, 256, held, 12288)
-        place(5, 256, S)
+        place(5, 256, S, sums=[(2, 3), (3, 4)])
         for c in range(5):
             place(c, 128, S)
         for c in (6, 7):

@@ -17,18 +17,35 @@ GELU = mybir.ActivationFunctionType.Gelu_apprx_tanh
 MULT = mybir.AluOpType.mult
 
 P = 128
-PASSES = K // 512
+PACK = 4
+PASSES = K // (P * PACK)
 TILES = M // P
 N = 128
-PIECES = [(0, 128), (128, 256), (256, 512)]
-WINDOWS = 8
+GROUPS = S // N
+QUADRANT = 32
+BANKS = 8
+
+PIECES = [(0, N), (N, 2 * N), (2 * N, S)]
+NARROW = range(0, 5)
+AHEAD_OF_PIECE_1 = 3
+FIRST_WINDOWS = 3
 HALF = M // 2
 
+RAW_AT = [[PACK * 4 * (PASSES * j0 + a * (j1 - j0)) for a in range(PASSES)] for j0, j1 in PIECES]
+WINDOW_BYTES = 4 * T
+GROUPED_BYTES = 2 * PACK * N
+LAP = 64
+GROUPED_01_AT = WINDOW_BYTES - LAP
+WINDOW_5_AT = GROUPED_01_AT + GROUPED_BYTES - LAP
+WINDOW_6_AT = WINDOW_5_AT + WINDOW_BYTES
+GROUPED_1_AT = WINDOW_6_AT + WINDOW_BYTES - LAP
+WINDOW_7_AT = GROUPED_1_AT + PASSES * GROUPED_BYTES - LAP
 
-def interleave(copy, dst, src):
+
+def interleave(copy, grouped, raw):
     copy(
-        out=dst.rearrange("p (c i) t -> p c t i", i=4),
-        in_=src.rearrange("p t (c i) -> p c t i", i=4),
+        out=grouped.rearrange("p (c u) i -> p c i u", u=4),
+        in_=raw.rearrange("p i (c u) -> p c i u", u=4),
     )
 
 
@@ -36,144 +53,157 @@ def tile_list_hscat_gelu_kernel(tc, x, w_words, w_scales, b, wgo, offs, out):
     nc = tc.nc
     with ExitStack() as ctx:
         keep = ctx.enter_context(tc.tile_pool(name="keep", bufs=1))
-        psum = ctx.enter_context(tc.psum_pool(name="psum", bufs=8))
-        late = ctx.enter_context(tc.tile_pool(name="late", bufs=1))
-        held = ctx.enter_context(tc.tile_pool(name="held", bufs=1))
+        psum = ctx.enter_context(tc.psum_pool(name="psum", bufs=BANKS))
+        chained = ctx.enter_context(tc.tile_pool(name="chained", bufs=1))
+        staged = ctx.enter_context(tc.tile_pool(name="staged", bufs=1))
 
         offsets = keep.tile([P, S // 16], U16, name="offsets")
-        planes = [keep.tile([P, PASSES, HALF], U8, name=f"planes{h}", align_bytes=64) for h in range(2)]
-        codes = [keep.tile([P, PASSES, N], U32, name=f"codes{g}", align_bytes=64) for g in range(S // N)]
-        scales = [keep.tile([P, PASSES, N], U8, name=f"scales{g}", align_bytes=64) for g in range(S // N)]
-        wins = [keep.tile([P, T], F32, name=f"win{w}") for w in range(3)]
-        warm = keep.tile([P, 1], F32, name="warm")
-        b_rows = keep.tile([P, 32], F32, name="b_rows", align_bytes=64)
+        w_planes = [keep.tile([P, PASSES, HALF], U8, name=f"w_plane{h}", align_bytes=64) for h in range(2)]
+        x_codes = [keep.tile([P, PASSES, N], U32, name=f"x_codes{g}", align_bytes=64) for g in range(GROUPS)]
+        x_planes = [keep.tile([P, PASSES, N], U8, name=f"x_plane{g}", align_bytes=64) for g in range(GROUPS)]
+        windows = [keep.tile([P, T], F32, name=f"window{c}") for c in range(FIRST_WINDOWS)]
+        warm = keep.tile([1, 1], F32, name="warm")
+        b_rows = keep.tile([P, QUADRANT], F32, name="b_rows", align_bytes=64)
         weights = keep.tile([P, S], F32, name="weights", align_bytes=64)
 
-        x_view = x.rearrange("(a p i) j -> a p i j", a=PASSES, i=4)
-        w_view = w_words.bitcast(I32).rearrange("a p n -> p a n")
-        s_view = w_scales.bitcast(I32).rearrange("a q n -> q a n")
-        planes_i32 = [half[:].rearrange("p a n -> p (a n)").bitcast(I32) for half in planes]
+        x_view = x.rearrange("(a p i) j -> a p i j", a=PASSES, i=PACK)
+        words_view = w_words.bitcast(I32).rearrange("a p n -> p a n")
+        scales_view = w_scales.bitcast(I32).rearrange("a q n -> q a n")
 
         def load_scales(h):
-            rows = planes_i32[h].rearrange("p (a n) -> p a n", a=PASSES)
-            for q in (0, 2, 1, 3):
+            as_words = w_planes[h][:].rearrange("p a n -> p (a n)").bitcast(I32)
+            rows = as_words.rearrange("p (a n) -> p a n", a=PASSES)
+            for u in (0, 2, 1, 3):
                 nc.sync.dma_start(
-                    out=rows[32 * q : 32 * q + 4], in_=s_view[4 * q : 4 * q + 4, :, h * HALF // 4 : (h + 1) * HALF // 4]
+                    out=rows[QUADRANT * u : QUADRANT * u + 4],
+                    in_=scales_view[4 * u : 4 * u + 4, :, h * HALF // 4 : (h + 1) * HALF // 4],
                 )
 
-        def load_x(n, a, offset):
+        raw = {}
+
+        def load_x(n, a):
             j0, j1 = PIECES[n]
-            raw = held.tile([P, 4, j1 - j0], F32, name=f"raw{n}{a}", offset=offset, align_bytes=64)
-            nc.sync.dma_start(out=raw[:], in_=x_view[a][:, :, j0:j1])
-            return raw
+            raw[n, a] = staged.tile([P, PACK, j1 - j0], F32, name=f"raw{n}{a}", offset=RAW_AT[n][a], align_bytes=64)
+            nc.sync.dma_start(out=raw[n, a][:], in_=x_view[a][:, :, j0:j1])
 
         words = {}
 
         def load_words(c0):
-            tile = keep.tile([P, PASSES, P], I32, name=f"words{c0}", align_bytes=64)
-            nc.sync.dma_start(out=tile[:], in_=w_view[:, :, c0 * P // 2 : (c0 + 2) * P // 2])
+            pair = keep.tile([P, PASSES, P], I32, name=f"words{c0}", align_bytes=64)
+            nc.sync.dma_start(out=pair[:], in_=words_view[:, :, c0 * P // 2 : (c0 + 2) * P // 2])
             for c in (c0, c0 + 1):
-                words[c] = tile[:, :, (c - c0) * P // 2 : (c - c0 + 1) * P // 2]
+                words[c] = pair[:, :, (c - c0) * P // 2 : (c - c0 + 1) * P // 2]
 
         def load_weights(j0, j1):
             nc.sync.dma_start(out=weights[:, j0:j1], in_=wgo[:, j0:j1])
 
         nc.vector.memset(b_rows[:], 0.0)
-        raw = [[load_x(0, 0, 0)]]
-        nc.sync.dma_start(out=b_rows[0:P:4, :], in_=b.rearrange("(c q j) -> q c j", c=TILES, q=4))
-        raw[0].append(load_x(0, 1, 2048))
+
+        load_x(0, 0)
+        nc.sync.dma_start(out=b_rows[3:P:4, :], in_=b.rearrange("(c u j) -> u c j", c=TILES, u=P // QUADRANT))
+        load_x(0, 1)
         load_scales(0)
         load_words(0)
         load_words(2)
-        load_weights(0, N)
+        load_weights(*PIECES[0])
         nc.sync.dma_start(offsets[:], offs)
-        for win in wins:
-            nc.vector.memset(win[:].bitcast(I32), 0)
-        raw.append([load_x(1, 0, 4096), load_x(1, 1, 6144)])
+        for window in windows:
+            nc.vector.memset(window[:].bitcast(I32), 0)
+        load_x(1, 0)
+        load_x(1, 1)
         load_words(4)
         load_scales(1)
-        load_weights(N, 2 * N)
+        load_weights(*PIECES[1])
         load_words(6)
-        raw.append([load_x(2, 0, 8192), load_x(2, 1, 12288)])
-        load_weights(2 * N, S)
+        load_x(2, 0)
+        load_x(2, 1)
+        load_weights(*PIECES[2])
 
-        nc.scalar.activation(out=warm[:], in_=wins[0][:, 0:1], func=GELU)
+        nc.scalar.activation(out=warm[:], in_=b_rows[0:1, 0:1], func=GELU)
 
-        def quantize(grouped, n, a0, a1):
+        def quantize(grouped, g, a0, a1):
             nc.vector.quantize_mx(
-                out=codes[n][:, a0:a1, :].rearrange("p a j -> p (a j)").bitcast(FP8X4),
-                scales=scales[n][:, a0:a1, :].rearrange("p a j -> p (a j)"),
-                in_=grouped.rearrange("p a j t -> p (a j t)"),
+                out=x_codes[g][:, a0:a1, :].rearrange("p a j -> p (a j)").bitcast(FP8X4),
+                scales=x_planes[g][:, a0:a1, :].rearrange("p a j -> p (a j)"),
+                in_=grouped.rearrange("p a j i -> p (a j i)"),
             )
 
-        def quantize_later(n, grouped):
-            for a in range(PASSES):
-                interleave(nc.scalar.copy, grouped[:, a], raw[n][a][:])
-            quantize(grouped[:], n, 0, PASSES)
+        grouped00 = keep.tile([P, 1, N, PACK], BF16, name="grouped00", align_bytes=64)
+        grouped01 = chained.tile([P, 1, N, PACK], BF16, name="grouped01", offset=GROUPED_01_AT, align_bytes=64)
+        interleave(nc.vector.tensor_copy, grouped00[:, 0], raw[0, 0][:])
+        bias = keep.tile([P, QUADRANT], F32, name="bias", align_bytes=64)
+        nc.vector.transpose(bias[:], b_rows[:])
+        quantize(grouped00[:], 0, 0, 1)
+        interleave(nc.vector.tensor_copy, grouped01[:, 0], raw[0, 1][:])
+        quantize(grouped01[:], 0, 1, 2)
 
-        firsts = [
-            keep.tile([P, 1, N, 4], BF16, name="grouped00", align_bytes=64),
-            late.tile([P, 1, N, 4], BF16, name="grouped01", offset=4032, align_bytes=64),
-        ]
-        interleave(nc.vector.tensor_copy, firsts[0][:, 0], raw[0][0][:])
-        b_turned = keep.tile([P, 32], F32, name="b_turned", align_bytes=64)
-        nc.vector.transpose(b_turned[:], b_rows[:])
-        quantize(firsts[0][:], 0, 0, 1)
-        interleave(nc.vector.tensor_copy, firsts[1][:, 0], raw[0][1][:])
-        quantize(firsts[1][:], 0, 1, 2)
+        def zero_window(engine, pool, offset):
+            window = pool.tile([P, T], F32, name=f"window{len(windows)}", offset=offset, align_bytes=64)
+            engine.memset(window[:].bitcast(I32), 0)
+            windows.append(window)
 
-        def late_window(offset, engine=nc.gpsimd, pool=late):
-            win = pool.tile([P, T], F32, name=f"win{len(wins)}", offset=offset, align_bytes=64)
-            engine.memset(win[:].bitcast(I32), 0)
-            wins.append(win)
-
-        def place(c, j0, j1, pool=keep, offset=None, sums=None):
-            val = pool.tile([P, j1 - j0], F32, name=f"val{c}_{j0}", offset=offset, align_bytes=64)
-            for g0, g1 in sums or [(j0 // N, j1 // N)]:
-                multiply(c, g0, g1, val[:, g0 * N - j0 : g1 * N - j0])
-            win = wins[c % WINDOWS]
-            nc.vector.tensor_tensor(win[:].indirect(offsets[:, j0 // 16 : j1 // 16]), val[:], weights[:, j0:j1], MULT)
-            if j1 == S:
-                nc.sync.dma_start(out=out[P * c : P * (c + 1), :], in_=win[:])
-
-        def multiply(c, g0, g1, val):
+        def project(c, groups, values):
             acc = psum.tile([P, S], F32, name="acc")
-            for g in sorted(range(g0, g1), key=lambda g: g == 2):
+            first = min(groups)
+            for g in groups:
                 for a in range(PASSES):
                     nc.tensor.matmul_mx(
-                        out=acc[:, (g - g0) * N : (g - g0 + 1) * N],
+                        out=acc[:, (g - first) * N : (g - first + 1) * N],
                         lhsT=words[c][:, a].bitcast(U8).bitcast(FP4X4),
-                        lhsT_scale=planes[c // 4][:, a, P * (c % 4) : P * (c % 4 + 1)],
-                        rhs=codes[g][:, a].bitcast(FP8X4),
-                        rhs_scale=scales[g][:, a],
+                        lhsT_scale=w_planes[c // 4][:, a, P * (c % 4) : P * (c % 4 + 1)],
+                        rhs=x_codes[g][:, a].bitcast(FP8X4),
+                        rhs_scale=x_planes[g][:, a],
                         start=(a == 0),
                         stop=(a == PASSES - 1),
                     )
-            nc.scalar.activation(out=val, in_=acc[:, 0 : (g1 - g0) * N], func=GELU, bias=b_turned[:, 4 * c : 4 * c + 1])
+            nc.scalar.activation(
+                out=values, in_=acc[:, 0 : len(groups) * N], func=GELU, bias=bias[:, 4 * c + 3 : 4 * c + 4]
+            )
 
-        late_window(0, nc.vector, held)
-        late_window(0)
-        late_window(4992)
-        for c in range(3):
-            place(c, 0, 128)
-        quantize_later(1, late.tile([P, PASSES, N, 4], BF16, name="grouped1", offset=13120, align_bytes=64))
-        late_window(9088)
-        late_window(15104)
-        place(3, 0, 128, held, 4096)
-        place(4, 0, 128, held, 6656)
-        place(5, 0, 256)
-        place(6, 0, 256)
-        grouped2 = keep.tile([P, 2, PASSES, N, 4], BF16, name="grouped2", align_bytes=64)
+        def place(c, sums, over=None):
+            j0, j1 = N * min(sums[0]), N * (max(sums[-1]) + 1)
+            if over is None:
+                values = keep.tile([P, j1 - j0], F32, name=f"values{c}_{j0}", align_bytes=64)
+            else:
+                at = RAW_AT[over[0]][over[1]]
+                values = staged.tile([P, j1 - j0], F32, name=f"values{c}_{j0}", offset=at, align_bytes=64)
+            for groups in sums:
+                project(c, groups, values[:, N * min(groups) - j0 : N * (max(groups) + 1) - j0])
+            nc.vector.tensor_tensor(
+                windows[c][:].indirect(offsets[:, j0 // 16 : j1 // 16]), values[:], weights[:, j0:j1], MULT
+            )
+            if j1 == S:
+                nc.sync.dma_start(out=out[P * c : P * (c + 1), :], in_=windows[c][:])
+
+        zero_window(nc.vector, staged, RAW_AT[0][0])
+        zero_window(nc.gpsimd, chained, 0)
+        zero_window(nc.gpsimd, chained, WINDOW_5_AT)
+        for c in NARROW[:AHEAD_OF_PIECE_1]:
+            place(c, [[0]])
+
+        grouped1 = chained.tile([P, PASSES, N, PACK], BF16, name="grouped1", offset=GROUPED_1_AT, align_bytes=64)
+        for a in range(PASSES):
+            interleave(nc.scalar.copy, grouped1[:, a], raw[1, a][:])
+        quantize(grouped1[:], 1, 0, PASSES)
+        zero_window(nc.gpsimd, chained, WINDOW_6_AT)
+        zero_window(nc.gpsimd, chained, WINDOW_7_AT)
+        for a, c in enumerate(NARROW[AHEAD_OF_PIECE_1:]):
+            place(c, [[0]], over=(1, a))
+        place(5, [[0, 1]])
+        place(6, [[0, 1]])
+
+        grouped2 = keep.tile([P, 2, PASSES, N, PACK], BF16, name="grouped2", align_bytes=64)
         for a in range(PASSES):
             nc.scalar.copy(
-                out=grouped2[:, :, a].rearrange("p h (c i) t -> p h c t i", i=4),
-                in_=raw[2][a][:].rearrange("p t (h c i) -> p h c t i", h=2, i=4),
+                out=grouped2[:, :, a].rearrange("p h (c u) i -> p h c i u", u=4),
+                in_=raw[2, a][:].rearrange("p i (h c u) -> p h c i u", h=2, u=4),
             )
         for h in range(2):
             quantize(grouped2[:, h], 2 + h, 0, PASSES)
-        place(7, 0, 256, held, 12288)
-        place(5, 256, S, sums=[(2, 3), (3, 4)])
-        for c in range(5):
-            place(c, 128, S)
-        for c in (6, 7):
-            place(c, 256, S)
+        place(7, [[0, 1]], over=(2, 1))
+
+        place(5, [[2], [3]])
+        for c in NARROW:
+            place(c, [[1, 3, 2]])
+        place(6, [[3, 2]])
+        place(7, [[3, 2]])

@@ -35,11 +35,14 @@ RAW_AT = [[PACK * 4 * (PASSES * j0 + a * (j1 - j0)) for a in range(PASSES)] for 
 WINDOW_BYTES = 4 * T
 GROUPED_BYTES = 2 * PACK * N
 LAP = 64
-GROUPED_01_AT = WINDOW_BYTES - LAP
-WINDOW_5_AT = GROUPED_01_AT + GROUPED_BYTES - LAP
+B_BYTES = 4 * QUADRANT
+B_ROWS_AT = WINDOW_BYTES - LAP
+WINDOW_5_AT = B_ROWS_AT + B_BYTES - LAP
 WINDOW_6_AT = WINDOW_5_AT + WINDOW_BYTES
 GROUPED_1_AT = WINDOW_6_AT + WINDOW_BYTES - LAP
 WINDOW_7_AT = GROUPED_1_AT + PASSES * GROUPED_BYTES - LAP
+GROUPED_00_AT = WINDOW_7_AT + WINDOW_BYTES
+WINDOW_3_AT = GROUPED_00_AT + GROUPED_BYTES - LAP
 
 
 def interleave(copy, grouped, raw):
@@ -63,7 +66,7 @@ def tile_list_hscat_gelu_kernel(tc, x, w_words, w_scales, b, wgo, offs, out):
         x_planes = [keep.tile([P, PASSES, N], U8, name=f"x_plane{g}", align_bytes=64) for g in range(GROUPS)]
         windows = [keep.tile([P, T], F32, name=f"window{c}") for c in range(FIRST_WINDOWS)]
         warm = keep.tile([1, 1], F32, name="warm")
-        b_rows = keep.tile([P, QUADRANT], F32, name="b_rows", align_bytes=64)
+        b_rows = chained.tile([P, QUADRANT], F32, name="b_rows", offset=B_ROWS_AT, align_bytes=64)
         weights = keep.tile([P, S], F32, name="weights", align_bytes=64)
 
         x_view = x.rearrange("(a p i) j -> a p i j", a=PASSES, i=PACK)
@@ -100,13 +103,13 @@ def tile_list_hscat_gelu_kernel(tc, x, w_words, w_scales, b, wgo, offs, out):
         nc.vector.memset(b_rows[:], 0.0)
 
         load_x(0, 0)
-        nc.sync.dma_start(out=b_rows[3:P:4, :], in_=b.rearrange("(c u j) -> u c j", c=TILES, u=P // QUADRANT))
         load_x(0, 1)
+        nc.sync.dma_start(out=b_rows[3:P:4, :], in_=b.rearrange("(c u j) -> u c j", c=TILES, u=P // QUADRANT))
         load_scales(0)
         load_words(0)
-        load_words(2)
         load_weights(*PIECES[0])
         nc.sync.dma_start(offsets[:], offs)
+        load_words(2)
         for window in windows:
             nc.vector.memset(window[:].bitcast(I32), 0)
         load_x(1, 0)
@@ -128,14 +131,14 @@ def tile_list_hscat_gelu_kernel(tc, x, w_words, w_scales, b, wgo, offs, out):
                 in_=grouped.rearrange("p a j i -> p (a j i)"),
             )
 
-        grouped00 = keep.tile([P, 1, N, PACK], BF16, name="grouped00", align_bytes=64)
-        grouped01 = chained.tile([P, 1, N, PACK], BF16, name="grouped01", offset=GROUPED_01_AT, align_bytes=64)
+        grouped00 = chained.tile([P, 1, N, PACK], BF16, name="grouped00", offset=GROUPED_00_AT, align_bytes=64)
+        grouped01 = keep.tile([P, 1, N, PACK], BF16, name="grouped01", align_bytes=64)
         interleave(nc.vector.tensor_copy, grouped00[:, 0], raw[0, 0][:])
-        bias = keep.tile([P, QUADRANT], F32, name="bias", align_bytes=64)
-        nc.vector.transpose(bias[:], b_rows[:])
         quantize(grouped00[:], 0, 0, 1)
         interleave(nc.vector.tensor_copy, grouped01[:, 0], raw[0, 1][:])
         quantize(grouped01[:], 0, 1, 2)
+        bias = chained.tile([P, QUADRANT], F32, name="bias", offset=GROUPED_00_AT, align_bytes=64)
+        nc.vector.transpose(bias[:], b_rows[:])
 
         def zero_window(engine, pool, offset):
             window = pool.tile([P, T], F32, name=f"window{len(windows)}", offset=offset, align_bytes=64)
@@ -146,15 +149,16 @@ def tile_list_hscat_gelu_kernel(tc, x, w_words, w_scales, b, wgo, offs, out):
             acc = psum.tile([P, S], F32, name="acc")
             first = min(groups)
             for g in groups:
-                for a in range(PASSES):
+                order = range(PASSES) if (c, g) == (0, 0) else range(PASSES - 1, -1, -1)
+                for step, a in enumerate(order):
                     nc.tensor.matmul_mx(
                         out=acc[:, (g - first) * N : (g - first + 1) * N],
                         lhsT=words[c][:, a].bitcast(U8).bitcast(FP4X4),
                         lhsT_scale=w_planes[c // 4][:, a, P * (c % 4) : P * (c % 4 + 1)],
                         rhs=x_codes[g][:, a].bitcast(FP8X4),
                         rhs_scale=x_planes[g][:, a],
-                        start=(a == 0),
-                        stop=(a == PASSES - 1),
+                        start=(step == 0),
+                        stop=(step == PASSES - 1),
                     )
             nc.scalar.activation(
                 out=values, in_=acc[:, 0 : len(groups) * N], func=GELU, bias=bias[:, 4 * c + 3 : 4 * c + 4]
@@ -175,7 +179,7 @@ def tile_list_hscat_gelu_kernel(tc, x, w_words, w_scales, b, wgo, offs, out):
             if j1 == S:
                 nc.sync.dma_start(out=out[P * c : P * (c + 1), :], in_=windows[c][:])
 
-        zero_window(nc.vector, staged, RAW_AT[0][0])
+        zero_window(nc.vector, chained, WINDOW_3_AT)
         zero_window(nc.gpsimd, chained, 0)
         zero_window(nc.gpsimd, chained, WINDOW_5_AT)
         for c in NARROW[:AHEAD_OF_PIECE_1]:

@@ -107,9 +107,9 @@ def tile_list_hscat_gelu_kernel(tc, x, w_words, w_scales, b, wgo, offs, out):
         nc.sync.dma_start(out=b_rows[3:P:4, :], in_=b.rearrange("(c u j) -> u c j", c=TILES, u=P // QUADRANT))
         load_scales(0)
         load_words(0)
+        load_words(2)
         load_weights(*PIECES[0])
         nc.sync.dma_start(offsets[:], offs)
-        load_words(2)
         for window in windows:
             nc.vector.memset(window[:].bitcast(I32), 0)
         load_x(1, 0)
@@ -197,11 +197,12 @@ def tile_list_hscat_gelu_kernel(tc, x, w_words, w_scales, b, wgo, offs, out):
         place(6, [[0, 1]])
 
         grouped2 = keep.tile([P, 2, PASSES, N, PACK], BF16, name="grouped2", align_bytes=64)
-        for a in range(PASSES):
-            nc.scalar.copy(
-                out=grouped2[:, :, a].rearrange("p h (c u) i -> p h c i u", u=4),
-                in_=raw[2, a][:].rearrange("p i (h c u) -> p h c i u", h=2, u=4),
-            )
+        nc.scalar.copy(
+            out=grouped2[:, :, 0].rearrange("p h (c u) i -> p h c i u", u=4),
+            in_=raw[2, 0][:].rearrange("p i (h c u) -> p h c i u", h=2, u=4),
+        )
+        for h in range(2):
+            interleave(nc.scalar.copy, grouped2[:, h, 1], raw[2, 1][:, :, h * N : (h + 1) * N])
         for h in range(2):
             quantize(grouped2[:, h], 2 + h, 0, PASSES)
         place(7, [[0, 1]], over=(2, 1))

@@ -24,6 +24,7 @@ N = 128
 GROUPS = S // N
 QUADRANT = 32
 BANKS = 8
+BURST = 256
 
 PIECES = [(0, N), (N, 2 * N), (2 * N, S)]
 NARROW = range(0, 5)
@@ -34,10 +35,10 @@ HALF = M // 2
 RAW_AT = [[PACK * 4 * (PASSES * j0 + a * (j1 - j0)) for a in range(PASSES)] for j0, j1 in PIECES]
 WINDOW_BYTES = 4 * T
 GROUPED_BYTES = 2 * PACK * N
-LAP = 64
+LAP = BURST
 B_BYTES = 4 * QUADRANT
-B_ROWS_AT = WINDOW_BYTES - LAP
-WINDOW_5_AT = B_ROWS_AT + B_BYTES - LAP
+B_ROWS_AT = WINDOW_BYTES - B_BYTES // 2
+WINDOW_5_AT = WINDOW_BYTES
 WINDOW_6_AT = WINDOW_5_AT + WINDOW_BYTES
 GROUPED_1_AT = WINDOW_6_AT + WINDOW_BYTES - LAP
 WINDOW_7_AT = GROUPED_1_AT + PASSES * GROUPED_BYTES - LAP
@@ -61,13 +62,13 @@ def tile_list_hscat_gelu_kernel(tc, x, w_words, w_scales, b, wgo, offs, out):
         staged = ctx.enter_context(tc.tile_pool(name="staged", bufs=1))
 
         offsets = keep.tile([P, S // 16], U16, name="offsets")
-        w_planes = [keep.tile([P, PASSES, HALF], U8, name=f"w_plane{h}", align_bytes=64) for h in range(2)]
+        w_planes = [keep.tile([P, PASSES, HALF], U8, name=f"w_plane{h}", align_bytes=BURST) for h in range(2)]
         x_codes = [keep.tile([P, PASSES, N], U32, name=f"x_codes{g}", align_bytes=64) for g in range(GROUPS)]
         x_planes = [keep.tile([P, PASSES, N], U8, name=f"x_plane{g}", align_bytes=64) for g in range(GROUPS)]
-        windows = [keep.tile([P, T], F32, name=f"window{c}") for c in range(FIRST_WINDOWS)]
+        windows = [keep.tile([P, T], F32, name=f"window{c}", align_bytes=BURST) for c in range(FIRST_WINDOWS)]
         warm = keep.tile([1, 1], F32, name="warm")
         b_rows = chained.tile([P, QUADRANT], F32, name="b_rows", offset=B_ROWS_AT, align_bytes=64)
-        weights = keep.tile([P, S], F32, name="weights", align_bytes=64)
+        weights = keep.tile([P, S], F32, name="weights", align_bytes=BURST)
 
         x_view = x.rearrange("(a p i) j -> a p i j", a=PASSES, i=PACK)
         words_view = w_words.bitcast(I32).rearrange("a p n -> p a n")
@@ -86,13 +87,13 @@ def tile_list_hscat_gelu_kernel(tc, x, w_words, w_scales, b, wgo, offs, out):
 
         def load_x(n, a):
             j0, j1 = PIECES[n]
-            raw[n, a] = staged.tile([P, PACK, j1 - j0], F32, name=f"raw{n}{a}", offset=RAW_AT[n][a], align_bytes=64)
+            raw[n, a] = staged.tile([P, PACK, j1 - j0], F32, name=f"raw{n}{a}", offset=RAW_AT[n][a], align_bytes=BURST)
             nc.sync.dma_start(out=raw[n, a][:], in_=x_view[a][:, :, j0:j1])
 
         words = {}
 
         def load_words(c0):
-            pair = keep.tile([P, PASSES, P], I32, name=f"words{c0}", align_bytes=64)
+            pair = keep.tile([P, PASSES, P], I32, name=f"words{c0}", align_bytes=BURST)
             nc.sync.dma_start(out=pair[:], in_=words_view[:, :, c0 * P // 2 : (c0 + 2) * P // 2])
             for c in (c0, c0 + 1):
                 words[c] = pair[:, :, (c - c0) * P // 2 : (c - c0 + 1) * P // 2]
@@ -141,7 +142,7 @@ def tile_list_hscat_gelu_kernel(tc, x, w_words, w_scales, b, wgo, offs, out):
         nc.vector.transpose(bias[:], b_rows[:])
 
         def zero_window(engine, pool, offset):
-            window = pool.tile([P, T], F32, name=f"window{len(windows)}", offset=offset, align_bytes=64)
+            window = pool.tile([P, T], F32, name=f"window{len(windows)}", offset=offset, align_bytes=BURST)
             engine.memset(window[:].bitcast(I32), 0)
             windows.append(window)
 

from contextlib import ExitStack

import concourse.mybir as mybir

K, M, T, S = 1024, 1024, 1024, 512
FLOPS = 2 * K * M * S

F32 = mybir.dt.float32
BF16 = mybir.dt.bfloat16
I32 = mybir.dt.int32
U32 = mybir.dt.uint32
U16 = mybir.dt.uint16
U8 = mybir.dt.uint8
FP8X4 = mybir.dt.float8_e4m3fn_x4
FP4X4 = mybir.dt.float4_e2m1fn_x4
GELU = mybir.ActivationFunctionType.Gelu_apprx_tanh
MULT = mybir.AluOpType.mult

P = 128
PACK = 4
PASSES = K // (P * PACK)
TILES = M // P
N = 128
GROUPS = S // N
QUADRANT = 32
BANKS = 8
BURST = 256

PIECES = [(0, N), (N, 2 * N), (2 * N, S)]
NARROW = range(0, 5)
AHEAD_OF_PIECE_1 = 3
FIRST_WINDOWS = 3
HALF = M // 2

RAW_AT = [[PACK * 4 * (PASSES * j0 + a * (j1 - j0)) for a in range(PASSES)] for j0, j1 in PIECES]
WINDOW_BYTES = 4 * T
GROUPED_BYTES = 2 * PACK * N
LAP = BURST
B_BYTES = 4 * QUADRANT
B_ROWS_AT = WINDOW_BYTES - B_BYTES // 2
WINDOW_5_AT = WINDOW_BYTES
WINDOW_6_AT = WINDOW_5_AT + WINDOW_BYTES
GROUPED_1_AT = WINDOW_6_AT + WINDOW_BYTES - LAP
WINDOW_7_AT = GROUPED_1_AT + PASSES * GROUPED_BYTES - LAP
GROUPED_00_AT = WINDOW_7_AT + WINDOW_BYTES
WINDOW_3_AT = GROUPED_00_AT + GROUPED_BYTES - LAP


def interleave(copy, grouped, raw):
    copy(
        out=grouped.rearrange("p (c u) i -> p c i u", u=4),
        in_=raw.rearrange("p i (c u) -> p c i u", u=4),
    )


def tile_list_hscat_gelu_kernel(tc, x, w_words, w_scales, b, wgo, offs, out):
    nc = tc.nc
    with ExitStack() as ctx:
        keep = ctx.enter_context(tc.tile_pool(name="keep", bufs=1))
        psum = ctx.enter_context(tc.psum_pool(name="psum", bufs=BANKS))
        chained = ctx.enter_context(tc.tile_pool(name="chained", bufs=1))
        staged = ctx.enter_context(tc.tile_pool(name="staged", bufs=1))

        offsets = keep.tile([P, S // 16], U16, name="offsets")
        w_planes = [keep.tile([P, PASSES, HALF], U8, name=f"w_plane{h}", align_bytes=BURST) for h in range(2)]
        x_codes = [keep.tile([P, PASSES, N], U32, name=f"x_codes{g}", align_bytes=64) for g in range(GROUPS)]
        x_planes = [keep.tile([P, PASSES, N], U8, name=f"x_plane{g}", align_bytes=64) for g in range(GROUPS)]
        windows = [keep.tile([P, T], F32, name=f"window{c}", align_bytes=BURST) for c in range(FIRST_WINDOWS)]
        warm = keep.tile([1, 1], F32, name="warm")
        b_rows = chained.tile([P, QUADRANT], F32, name="b_rows", offset=B_ROWS_AT, align_bytes=64)
        weights = keep.tile([P, S], F32, name="weights", align_bytes=BURST)

        x_view = x.rearrange("(a p i) j -> a p i j", a=PASSES, i=PACK)
        words_view = w_words.bitcast(I32).rearrange("a p n -> p a n")
        scales_view = w_scales.bitcast(I32).rearrange("a q n -> q a n")

        def load_scales(h):
            as_words = w_planes[h][:].rearrange("p a n -> p (a n)").bitcast(I32)
            rows = as_words.rearrange("p (a n) -> p a n", a=PASSES)
            for u in (0, 2, 1, 3):
                nc.sync.dma_start(
                    out=rows[QUADRANT * u : QUADRANT * u + 4],
                    in_=scales_view[4 * u : 4 * u + 4, :, h * HALF // 4 : (h + 1) * HALF // 4],
                )

        raw = {}

        def load_x(n, a):
            j0, j1 = PIECES[n]
            raw[n, a] = staged.tile([P, PACK, j1 - j0], F32, name=f"raw{n}{a}", offset=RAW_AT[n][a], align_bytes=BURST)
            nc.sync.dma_start(out=raw[n, a][:], in_=x_view[a][:, :, j0:j1])

        words = {}

        def load_words(c0):
            pair = keep.tile([P, PASSES, P], I32, name=f"words{c0}", align_bytes=BURST)
            nc.sync.dma_start(out=pair[:], in_=words_view[:, :, c0 * P // 2 : (c0 + 2) * P // 2])
            for c in (c0, c0 + 1):
                words[c] = pair[:, :, (c - c0) * P // 2 : (c - c0 + 1) * P // 2]

        def load_weights(j0, j1):
            nc.sync.dma_start(out=weights[:, j0:j1], in_=wgo[:, j0:j1])

        nc.vector.memset(b_rows[:], 0.0)

        load_x(0, 0)
        load_x(0, 1)
        nc.sync.dma_start(out=b_rows[3:P:4, :], in_=b.rearrange("(c u j) -> u c j", c=TILES, u=P // QUADRANT))
        load_scales(0)
        load_words(0)
        load_words(2)
        load_weights(*PIECES[0])
        nc.sync.dma_start(offsets[:], offs)
        for window in windows:
            nc.vector.memset(window[:].bitcast(I32), 0)
        load_x(1, 0)
        load_x(1, 1)
        load_words(4)
        load_scales(1)
        load_weights(*PIECES[1])
        load_words(6)
        load_x(2, 0)
        load_x(2, 1)
        load_weights(*PIECES[2])

        nc.scalar.activation(out=warm[:], in_=b_rows[0:1, 0:1], func=GELU)

        def quantize(grouped, g, a0, a1):
            nc.vector.quantize_mx(
                out=x_codes[g][:, a0:a1, :].rearrange("p a j -> p (a j)").bitcast(FP8X4),
                scales=x_planes[g][:, a0:a1, :].rearrange("p a j -> p (a j)"),
                in_=grouped.rearrange("p a j i -> p (a j i)"),
            )

        grouped00 = chained.tile([P, 1, N, PACK], BF16, name="grouped00", offset=GROUPED_00_AT, align_bytes=64)
        grouped01 = keep.tile([P, 1, N, PACK], BF16, name="grouped01", align_bytes=64)
        interleave(nc.vector.tensor_copy, grouped00[:, 0], raw[0, 0][:])
        quantize(grouped00[:], 0, 0, 1)
        interleave(nc.vector.tensor_copy, grouped01[:, 0], raw[0, 1][:])
        quantize(grouped01[:], 0, 1, 2)
        bias = chained.tile([P, QUADRANT], F32, name="bias", offset=GROUPED_00_AT, align_bytes=64)
        nc.vector.transpose(bias[:], b_rows[:])

        def zero_window(engine, pool, offset):
            window = pool.tile([P, T], F32, name=f"window{len(windows)}", offset=offset, align_bytes=BURST)
            engine.memset(window[:].bitcast(I32), 0)
            windows.append(window)

        def project(c, groups, values):
            acc = psum.tile([P, S], F32, name="acc")
            first = min(groups)
            for g in groups:
                order = range(PASSES) if (c, g) == (0, 0) else range(PASSES - 1, -1, -1)
                for step, a in enumerate(order):
                    nc.tensor.matmul_mx(
                        out=acc[:, (g - first) * N : (g - first + 1) * N],
                        lhsT=words[c][:, a].bitcast(U8).bitcast(FP4X4),
                        lhsT_scale=w_planes[c // 4][:, a, P * (c % 4) : P * (c % 4 + 1)],
                        rhs=x_codes[g][:, a].bitcast(FP8X4),
                        rhs_scale=x_planes[g][:, a],
                        start=(step == 0),
                        stop=(step == PASSES - 1),
                    )
            nc.scalar.activation(
                out=values, in_=acc[:, 0 : len(groups) * N], func=GELU, bias=bias[:, 4 * c + 3 : 4 * c + 4]
            )

        def place(c, sums, over=None):
            j0, j1 = N * min(sums[0]), N * (max(sums[-1]) + 1)
            if over is None:
                values = keep.tile([P, j1 - j0], F32, name=f"values{c}_{j0}", align_bytes=64)
            else:
                at = RAW_AT[over[0]][over[1]]
                values = staged.tile([P, j1 - j0], F32, name=f"values{c}_{j0}", offset=at, align_bytes=64)
            for groups in sums:
                project(c, groups, values[:, N * min(groups) - j0 : N * (max(groups) + 1) - j0])
            nc.vector.tensor_tensor(
                windows[c][:].indirect(offsets[:, j0 // 16 : j1 // 16]), values[:], weights[:, j0:j1], MULT
            )
            if j1 == S:
                nc.sync.dma_start(out=out[P * c : P * (c + 1), :], in_=windows[c][:])

        zero_window(nc.vector, chained, WINDOW_3_AT)
        zero_window(nc.gpsimd, chained, 0)
        zero_window(nc.gpsimd, chained, WINDOW_5_AT)
        for c in NARROW[:AHEAD_OF_PIECE_1]:
            place(c, [[0]])

        grouped1 = chained.tile([P, PASSES, N, PACK], BF16, name="grouped1", offset=GROUPED_1_AT, align_bytes=64)
        for a in range(PASSES):
            interleave(nc.scalar.copy, grouped1[:, a], raw[1, a][:])
        quantize(grouped1[:], 1, 0, PASSES)
        zero_window(nc.gpsimd, chained, WINDOW_6_AT)
        zero_window(nc.gpsimd, chained, WINDOW_7_AT)
        for a, c in enumerate(NARROW[AHEAD_OF_PIECE_1:]):
            place(c, [[0]], over=(1, a))
        place(5, [[0, 1]])
        place(6, [[0, 1]])

        grouped2 = keep.tile([P, 2, PASSES, N, PACK], BF16, name="grouped2", align_bytes=64)
        nc.scalar.copy(
            out=grouped2[:, :, 0].rearrange("p h (c u) i -> p h c i u", u=4),
            in_=raw[2, 0][:].rearrange("p i (h c u) -> p h c i u", h=2, u=4),
        )
        for h in range(2):
            interleave(nc.scalar.copy, grouped2[:, h, 1], raw[2, 1][:, :, h * N : (h + 1) * N])
        for h in range(2):
            quantize(grouped2[:, h], 2 + h, 0, PASSES)
        place(7, [[0, 1]], over=(2, 1))

        place(5, [[2], [3]])
        for c in NARROW:
            place(c, [[1, 3, 2]])
        place(6, [[3, 2]])
        place(7, [[3, 2]])
